import numpy as np
import ml_dtypes


def mxq(x, axis, fmt="e4m3"):
    dtype, down = {"e4m3": (ml_dtypes.float8_e4m3fn, 7), "e5m2": (ml_dtypes.float8_e5m2, 14)}[fmt]
    v = np.moveaxis(np.asarray(x, np.float32).astype(ml_dtypes.bfloat16).astype(np.float64), axis, -1)
    blocks = v.reshape(v.shape[:-1] + (-1, 32))
    amax = np.abs(blocks).max(-1, keepdims=True)
    byte = np.maximum(np.where(amax > 0, np.frexp(amax)[1] - 1 + 127, 0) - down, 1)
    scale = np.exp2(byte - 127.0)
    codes = (blocks / scale).astype(np.float32).astype(dtype).astype(np.float64)
    return np.moveaxis((codes * scale).reshape(v.shape), -1, axis)


WIDE = False


def mx_kscale(k):
    if not WIDE:
        return np.ones(k)
    levels = np.array([10, -10, 5, -5, 0])
    if k % 512:
        return np.exp2(np.random.permutation(np.resize(levels, k // 32))).repeat(32)
    a = np.empty((k // 512, 16))
    for p in range(k // 512):
        a[p, :8] = np.random.permutation(np.resize(levels, 8))
        for g in range(8):
            far = levels[np.abs(levels - a[p, g]) >= 10]
            a[p, g + 8] = far[np.random.randint(len(far))]
    return np.exp2(a.ravel()).repeat(32)


BF16 = ml_dtypes.bfloat16


def bf(x):
    return np.asarray(x, np.float32).astype(BF16)


def f64(x):
    return np.asarray(x).astype(np.float64)


E2M1 = np.array([0.0, 0.5, 1.0, 1.5, 2.0, 3.0, 4.0, 6.0, -0.0, -0.5, -1.0, -1.5, -2.0, -3.0, -4.0, -6.0])


def pack_weight(w, fmt):
    k, n = w.shape
    w = f64(bf(w)).reshape(k // 32, 32, n)
    amax = np.abs(w).max(1)
    if fmt == "e4m3":
        byte = np.frexp(amax)[1] - 1 + 127 - 7
    else:
        mant, ex = np.frexp(amax / 6.0)
        byte = np.where(mant > 0.5, ex, ex - 1) + 127
    byte = np.clip(np.where(amax > 0, byte, 1), 1, 254)
    scaled = (w * np.exp2(127.0 - byte)[:, None, :]).reshape(k, n).astype(np.float32)
    by_word = np.ascontiguousarray(scaled.reshape(k // 512, 128, 4, n).transpose(0, 1, 3, 2))
    if fmt == "e4m3":
        words = by_word.astype(ml_dtypes.float8_e4m3fn).view(np.uint8)
    else:
        c = by_word.astype(ml_dtypes.float4_e2m1fn).view(np.uint8) & 0xF
        words = c[..., 0::2] | (c[..., 1::2] << 4)
    return np.ascontiguousarray(words), np.ascontiguousarray(byte.astype(np.uint8).reshape(k // 512, 16, n))


def unpack_weight(words, scales, fmt):
    g, p, n, _ = words.shape
    if fmt == "e4m3":
        vals = np.ascontiguousarray(words).view(ml_dtypes.float8_e4m3fn).astype(np.float64)
    else:
        nib = np.empty((g, p, n, 4), np.uint8)
        nib[..., 0::2] = words & 0xF
        nib[..., 1::2] = words >> 4
        vals = E2M1[nib]
    vals = vals * np.repeat(np.exp2(scales.astype(np.float64) - 127.0), 8, axis=1)[..., None]
    return vals.transpose(0, 1, 3, 2).reshape(g * 512, n)
def pack4(w):
    words, scales = pack_weight(w, "e2m1")
    return words.reshape(words.shape[0], 128, -1), scales


def unpack4(words, scales):
    return unpack_weight(words.reshape(words.shape[0], 128, -1, 2), scales, "e2m1")


L, M, E, P, D = 1536, 1024, 1024, 512, 1024


def draw0():
    s = mx_kscale(M)
    u = mx_kscale(P)
    t = mx_kscale(E)
    x = np.random.standard_normal((L, M)) * s
    cinv = np.random.standard_normal((M, E)) / np.sqrt(M) / s[:, None] * t
    cinv_words, cinv_scales = pack4(cinv)
    offset = 0.4 * np.random.standard_normal(E) * t
    modes = np.random.standard_normal((D, P)) * u
    samp = np.random.standard_normal((P, E)) / np.sqrt(P) / E ** 0.25 / u[:, None] / t
    taper = 1 + 0.1 * np.random.standard_normal(E)
    norm = (1 + 0.1 * np.random.standard_normal(D)) / E ** 0.25
    return {"x": bf(x), "cinv_words": cinv_words, "cinv_scales": cinv_scales,
            "offset": bf(offset), "modes": bf(modes), "samp": bf(samp),
            "taper": bf(taper), "norm": bf(norm)}


def core(x, cinv_words, cinv_scales, offset, modes, samp, taper, norm):
    cinv = unpack4(cinv_words, cinv_scales)
    y = (mxq(f64(x), 1, "e4m3") @ cinv) + f64(offset)
    a = (mxq(f64(modes), 1, "e4m3") @ mxq(f64(samp), 0, "e4m3")) * f64(taper)
    z = mxq(y, 1, "e4m3") @ mxq(a, 1, "e4m3").T
    return z * f64(norm)


def e4m3fn_bytes(y):
    return np.clip(np.asarray(y, np.float64), -448.0, 448.0).astype(np.float32).astype(ml_dtypes.float8_e4m3fn).view(np.uint8)


def e4m3fn_values(b):
    return np.asarray(b, np.uint8).view(ml_dtypes.float8_e4m3fn).astype(np.float64)


def setup_inputs():
    d = draw0()
    x0 = np.asarray(d['x']).astype(np.float64)
    s = (np.max(np.abs(x0), axis=(0,), keepdims=True) / 448.0).astype(np.float32)
    out = {}
    for k, v in d.items():
        if k == 'x':
            out['x_bytes'] = e4m3fn_bytes(x0 / s.astype(np.float64))
            out['x_scale'] = s
        else:
            out[k] = v
    return out


def reference(x_bytes, x_scale, cinv_words, cinv_scales, offset, modes, samp, taper, norm):
    return core(e4m3fn_values(x_bytes) * x_scale.astype(np.float64), cinv_words, cinv_scales, offset, modes, samp, taper, norm)

@@ -1,0 +1,313 @@
+from contextlib import ExitStack
+
+import concourse.mybir as mybir
+from concourse.masks import make_identity
+
+L, M, E, P, D = 1536, 1024, 1024, 512, 1024
+FLOPS = 2 * L * M * E + 2 * D * P * E + 2 * L * E * D
+
+F32 = mybir.dt.float32
+BF16 = mybir.dt.bfloat16
+U32 = mybir.dt.uint32
+I32 = mybir.dt.int32
+U8 = mybir.dt.uint8
+FP8 = mybir.dt.float8_e4m3fn
+FP8X4 = mybir.dt.float8_e4m3fn_x4
+FP4X4 = mybir.dt.float4_e2m1fn_x4
+ACT = mybir.ActivationFunctionType
+ALU = mybir.AluOpType
+
+PAIR = (("y", 2, 0), ("y", 2, 1),)
+
+ORDER = """
+TT000 TT001 SI00 SI01 CP TX00 SI02 CSP SI03 XS000 SQ0 XS001 XQ000 TT010 
+TM0 SI10 XQ001 SI11 TT011 MS00 MS01 MQ00 TT100 TX01 SI12 SI13 MQ01 TT101 
+XS010 AM000 AM001 XS011 AM002 XQ010 AS000 TM1 XQ011 SQ1 AS001 TT110 AS002 AM003 
+AM010 AS003 AM011 TT111 AM012 AS010 AS011 AM013 AI00 AS012 YM000 AS013 YM001 YM002 
+TT200 YS000 YS001 YM003 AQ00 YS002 YM010 AI01 YS003 YM011 MS10 YM012 MS11 YI00 
+YS010 TX10 YS011 AQ01 YS012 YM013 YQ00 XS100 MQ10 MQ11 XS101 XQ100 AM100 YS013 
+XQ101 TX11 TT201 AS100 AM101 XS110 YI01 AM102 AM103 XS111 AS101 TX20 XQ110 XQ111 
+AS102 YQ01 AS103 AM110 TT210 AM111 AS110 AM112 ZM000 AS111 AI10 AM113 AS112 ZM010 
+AS113 YM100 TT211 YM101 XS200 XS201 YM102 AQ10 ZM020 YS100 AI11 TX21 YS101 YS102 
+XQ200 XS210 YM103 AQ11 YM110 XS211 XQ201 XQ210 YS103 YM111 XQ211 ZT000 YS110 YM112 
+YI10 YS111 YM113 ZM030 YS112 YM200 YS113 ZT010 YS200 YM201 YQ10 YM202 YI11 YS201 
+YM203 ZM001 YS202 ZT020 YM210 YQ11 YS203 YM211 ZT030 ZM011 YS210 YI20 YM212 YS211 
+ZT001 YM213 YQ20 ZM021 YS212 ZT011 ZM031 YS213 ZT021 ZM100 ZT031 ZM110 YI21 ZM120 
+ZT100 YQ21 ZM130 ZT110 ZT120 ZM101 ZT130 ZM111 ZM121 ZT101 ZT111 ZM131 ZT121 ZM200 
+ZT131 ZM210 ZT200 ZM220 ZM230 ZT210 ZT220 ZM201 ZT230 ZM211 ZT201 ZM221 ZT211 ZM231 
+ZT221 ZT231
+"""
+
+
+def tile_coupling_compensated_beams_s11_kernel(
+    tc, x_bytes, x_scale, cinv_words, cinv_scales, offset, modes, samp, taper, norm, out
+):
+    nc = tc.nc
+    with ExitStack() as ctx:
+        ctx.enter_context(tc.manual_schedule())
+        keep = ctx.enter_context(tc.tile_pool(name="keep", bufs=1))
+        work = ctx.enter_context(tc.tile_pool(name="work", bufs=3))
+        psum = ctx.enter_context(tc.psum_pool(name="psum", bufs=2))
+
+        scales_raw = keep.tile([128, 2, E], U8, align_bytes=64)
+        nc.vector.memset(scales_raw[:].bitcast(I32), 0)
+        vecs = keep.tile([128, 128], BF16, align_bytes=64)
+        nc.gpsimd.memset(vecs[:], 0.0)
+        ident = keep.tile([128, 128], F32, align_bytes=64)
+        make_identity(nc, ident[:])
+        ident_b = keep.tile([128, 128], BF16, align_bytes=64)
+        make_identity(nc, ident_b[:])
+
+        xsc = keep.tile([128, M], F32, align_bytes=64)
+        nc.scalar.dma_start(out=xsc[:], in_=x_scale.rearrange("o k -> (o k)").partition_broadcast(128))
+        for v, vec in enumerate((offset, taper)):
+            for eg in range(2):
+                row = 8 * v + 4 * eg
+                nc.scalar.dma_start(
+                    out=vecs[row : row + 4, :].rearrange("t (q r) -> t q r", r=8),
+                    in_=vec[512 * eg : 512 * (eg + 1)].rearrange("(q t r) -> t q r", t=4, r=8),
+                )
+        x_rows = x_bytes.rearrange("(c p i) k -> c p i k", p=128, i=4)
+        x_raw = {}
+
+        def load_x(c, h):
+            x_in = keep.tile([128, 2, M], U8, name=f"x_raw_{c}{h}", align_bytes=64)
+            nc.sync.dma_start(out=x_in[:], in_=x_rows[c, :, 2 * h : 2 * h + 2, :])
+            x_raw[c, h] = x_in
+
+        words_raw = keep.tile([128, 2, 2 * E], U8, align_bytes=64)
+        samp_raw = keep.tile([128, 4, E], BF16, align_bytes=64)
+        samp_rows = samp.rearrange("(p j) e -> p j e", j=4)
+        modes_raw = [keep.tile([128, 4, P], BF16, name=f"modes_raw_{j}", align_bytes=64) for j in range(2)]
+
+        def load_modes(j):
+            nc.sync.dma_start(out=modes_raw[j][:], in_=modes[512 * j : 512 * (j + 1), :].rearrange("(i p) k -> p i k", p=128))
+
+        def load_samp(eg):
+            nc.sync.dma_start(out=samp_raw[:, :, 512 * eg : 512 * (eg + 1)], in_=samp_rows[:, :, 512 * eg : 512 * (eg + 1)])
+
+        load_x(0, 0)
+        for q in range(4):
+            nc.sync.dma_start(
+                out=scales_raw[32 * q : 32 * q + 4, :, :].bitcast(I32),
+                in_=cinv_scales[:, 4 * q : 4 * q + 4, :].rearrange("g r n -> r g n").bitcast(I32),
+            )
+        load_samp(0)
+        nc.sync.dma_start(out=words_raw[:].bitcast(I32), in_=cinv_words.rearrange("g p n -> p g n").bitcast(I32))
+        load_modes(0)
+        load_x(0, 1)
+        load_samp(1)
+        load_x(1, 0)
+        load_x(1, 1)
+        load_modes(1)
+        load_x(2, 0)
+        load_x(2, 1)
+        norm_b = keep.tile([128, D], BF16, align_bytes=64)
+        nc.sync.dma_start(out=norm_b[:], in_=norm.partition_broadcast(128))
+
+        vec_t = psum.tile([128, 128], BF16, tag="tr", bufs=2)
+        nc.tensor.transpose(vec_t[:], vecs[:], ident_b[:])
+        cols = keep.tile([128, 16], F32, align_bytes=64)
+        nc.scalar.copy(cols[:], vec_t[:, 0:16])
+
+        words = keep.tile([128, 2, 2 * E], U8, align_bytes=64)
+        scales = keep.tile([128, 2, E], U8, align_bytes=64)
+
+        def permute(dst, src, w):
+            n = 64 * w
+            for g in range(2):
+                for eg in range(2):
+                    d32 = dst[:, g, :].bitcast(I32)[:, n * eg : n * (eg + 1)]
+                    s32 = src[:, g, :].bitcast(I32)[:, n * eg : n * (eg + 1)]
+                    nc.vector.tensor_copy(
+                        out=d32.rearrange("p (t q w) -> p t q w", t=4, w=w),
+                        in_=s32.rearrange("p (q t w) -> p t q w", t=4, w=w),
+                    )
+
+        def CP():
+            permute(words, words_raw, 4)
+
+        def CSP():
+            permute(scales, scales_raw, 2)
+
+        def pairs_of(names, width):
+            return (
+                {k: keep.tile([128, width], U32, name=f"{names}_codes_{'_'.join(str(i) for i in k)}", align_bytes=64) for k in KEYS[names]},
+                {k: keep.tile([128, width], U8, name=f"{names}_scales_{'_'.join(str(i) for i in k)}", align_bytes=64) for k in KEYS[names]},
+            )
+
+        KEYS = {
+            "x": [(c, g) for c in range(3) for g in range(2)],
+            "m": [(j,) for j in range(2)],
+            "s": [(eg,) for eg in range(2)],
+            "a": [(j, eg) for j in range(2) for eg in range(2)],
+            "y": [(c, eg) for c in range(3) for eg in range(2)],
+        }
+        xq, xqs = pairs_of("x", 512)
+        mq, mqs = pairs_of("m", 512)
+        sq, sqs = pairs_of("s", 512)
+        aq, aqs = pairs_of("a", 512)
+        yq, yqs = pairs_of("y", 512)
+        live = {}
+
+        def TT(c, h, i):
+            if i == 0:
+                xb_new = work.tile([128, 2, M], BF16, tag="xb", bufs=4, align_bytes=64)
+                live["xb", c, h] = xb_new
+            nc.vector.tensor_tensor(
+                out=live["xb", c, h][:, i, :], in0=x_raw[c, h][:, i, :].bitcast(FP8), in1=xsc[:], op=ALU.mult
+            )
+
+        def flip(key, w, k0):
+            pt = psum.tile([128, 2, 2, 128], F32, tag="tr", bufs=2)
+            for i in range(2):
+                for u in range(2):
+                    nc.tensor.transpose(pt[:, i, u, :], w[i][:, k0 + u : k0 + 256 : 2], ident[:])
+            live[key] = pt
+
+        def lift(key):
+            pt = live[key]
+            xi = work.tile([128, 256, 4], BF16, tag="xi", bufs=4, align_bytes=64)
+            nc.scalar.copy(
+                xi[:].rearrange("p n t -> p (n t)").bitcast(F32).rearrange("p (i r u) -> p i r u", i=2, u=2),
+                pt[:].rearrange("p i u r -> p i r u"),
+            )
+            live[key] = xi
+
+        def quant(src, codes, planes):
+            nc.vector.quantize_mx(out=codes.bitcast(FP8X4), scales=planes, in_=src)
+
+        def TX(c, h):
+            xb = live["xb", c, h]
+            for g in range(2):
+                flip(("x", c, h, g), [xb[:, i, :].bitcast(F32) for i in range(2)], 256 * g)
+
+        def XS(c, h, g):
+            lift(("x", c, h, g))
+
+        def XQ(c, h, g):
+            s = slice(256 * h, 256 * (h + 1))
+            quant(live["x", c, h, g][:].rearrange("p n t -> p (n t)"), xq[c, g][:, s], xqs[c, g][:, s])
+
+        def TM(j):
+            for b in range(2):
+                flip(("m", j, b), [modes_raw[j][:, 2 * b + i, :].bitcast(F32) for i in range(2)], 0)
+
+        def MS(j, b):
+            lift(("m", j, b))
+
+        def MQ(j, b):
+            s = slice(256 * b, 256 * (b + 1))
+            quant(live["m", j, b][:].rearrange("p n t -> p (n t)"), mq[j,][:, s], mqs[j,][:, s])
+
+        def SI(eg, t):
+            if t == 0:
+                si_new = work.tile([128, 512, 4], BF16, tag="si", bufs=2, align_bytes=64)
+                live["s", eg] = si_new
+            src = samp_raw[:, :, 512 * eg : 512 * (eg + 1)].rearrange("p j (q t r) -> p t q r j", t=4, r=8)
+            dst = live["s", eg][:].rearrange("p (t q r) j -> p t q r j", t=4, r=8)
+            nc.scalar.copy(dst[:, t], src[:, t])
+
+        def SQ(eg):
+            quant(live["s", eg][:].rearrange("p n j -> p (n j)"), sq[eg,][:], sqs[eg,][:])
+
+        def AM(j, eg, t):
+            acc = psum.tile([128, 512], F32, tag="acc", bufs=3)
+            s = slice(128 * t, 128 * (t + 1))
+            nc.tensor.matmul_mx(
+                out=acc[:], lhsT=sq[eg,][:, s].bitcast(FP8X4), lhsT_scale=sqs[eg,][:, s],
+                rhs=mq[j,][:].bitcast(FP8X4), rhs_scale=mqs[j,][:], start=True, stop=True,
+            )
+            live["a", j, eg, t] = acc
+
+        def YM(c, eg, t):
+            acc = psum.tile([128, 512], F32, tag="acc", bufs=3)
+            e0 = 512 * eg + 128 * t
+            for g in range(2):
+                nc.tensor.matmul_mx(
+                    out=acc[:], lhsT=words[:, g, 2 * e0 : 2 * (e0 + 128)].bitcast(FP4X4),
+                    lhsT_scale=scales[:, g, e0 : e0 + 128],
+                    rhs=xq[c, g][:].bitcast(FP8X4), rhs_scale=xqs[c, g][:],
+                    start=(g == 0), stop=(g == 1),
+                )
+            live["y", c, eg, t] = acc
+
+        def empty(kind, i, eg, t):
+            key = kind + "raw", i, eg
+            if t == 0:
+                raw_new = work.tile([128, 2048], BF16, tag="raw", bufs=4, align_bytes=64)
+                live[key] = raw_new
+            raw = live[key]
+            if (kind, i, eg) in PAIR:
+                dst = raw[:].rearrange("p (u n e) -> p u n e", u=2, e=2)[:, t // 2, :, t % 2]
+            else:
+                dst = raw[:, 512 * t : 512 * (t + 1)]
+            acc = live[kind, i, eg, t]
+            col = 4 * eg + t
+            if kind == "y":
+                nc.scalar.activation(out=dst, in_=acc[:], func=ACT.Identity, bias=cols[:, col : col + 1], scale=1.0)
+            else:
+                nc.scalar.activation(out=dst, in_=acc[:], func=ACT.Copy, scale=cols[:, 8 + col : 9 + col])
+
+        def AS(j, eg, t):
+            empty("a", j, eg, t)
+
+        def YS(c, eg, t):
+            empty("y", c, eg, t)
+
+        def weave(kind, i, eg):
+            raw = live[kind + "raw", i, eg]
+            lay = work.tile([128, 2048], BF16, tag="lay", bufs=4, align_bytes=64)
+            if (kind, i, eg) in PAIR:
+                nc.vector.tensor_copy(
+                    out=lay[:].bitcast(F32).rearrange("p (n u) -> p n u", u=2),
+                    in_=raw[:].bitcast(F32).rearrange("p (u n) -> p n u", u=2),
+                )
+            else:
+                nc.vector.tensor_copy(
+                    out=lay[:].rearrange("p (n t) -> p n t", t=4), in_=raw[:].rearrange("p (t n) -> p n t", t=4)
+                )
+            live[kind + "lay", i, eg] = lay
+
+        def AI(j, eg):
+            weave("a", j, eg)
+
+        def YI(c, eg):
+            weave("y", c, eg)
+
+        def AQ(j, eg):
+            quant(live["alay", j, eg][:], aq[j, eg][:], aqs[j, eg][:])
+
+        def YQ(c, eg):
+            quant(live["ylay", c, eg][:], yq[c, eg][:], yqs[c, eg][:])
+
+        out_rows = out.rearrange("(c p i) d -> c p i d", p=128, i=4)
+
+        def ZM(c, i, j):
+            acc = psum.tile([128, 512], F32, tag="z", bufs=3)
+            s = slice(128 * i, 128 * (i + 1))
+            for eg in range(2):
+                nc.tensor.matmul_mx(
+                    out=acc[:], lhsT=yq[c, eg][:, s].bitcast(FP8X4), lhsT_scale=yqs[c, eg][:, s],
+                    rhs=aq[j, eg][:].bitcast(FP8X4), rhs_scale=aqs[j, eg][:], start=(eg == 0), stop=(eg == 1),
+                )
+            live["z", c, i, j] = acc
+
+        def ZC(c, i, j):
+            zc = work.tile([128, 512], F32, tag="zc", bufs=3)
+            nc.scalar.copy(zc[:], live["z", c, i, j][:])
+            live["z", c, i, j] = zc
+
+        def ZT(c, i, j):
+            d0 = 512 * j
+            res = work.tile([128, 512], F32, tag="res", bufs=6)
+            engine = nc.gpsimd if (c, i, j) in () else nc.vector
+            engine.tensor_tensor(out=res[:], in0=live["z", c, i, j][:], in1=norm_b[:, d0 : d0 + 512], op=ALU.mult)
+            nc.sync.dma_start(out=out_rows[c, :, i, d0 : d0 + 512], in_=res[:])
+
+        ops = {
+            "TT": TT, "TX": TX, "XS": XS, "XQ": XQ, "TM": TM, "MS": MS, "MQ": MQ, "SI": SI, "SQ": SQ, "AM": AM, "AS": AS,
+            "AI": AI, "AQ": AQ, "YM": YM, "YS": YS, "YI": YI, "YQ": YQ, "ZM": ZM, "ZC": ZC, "ZT": ZT, "CP": CP, "CS": CSP,
+        }
+        for op in ORDER.split():
+            ops[op[:2]](*[int(v) for v in op[2:].replace("P", "")])

@@ -17,25 +17,25 @@ FP4X4 = mybir.dt.float4_e2m1fn_x4
 ACT = mybir.ActivationFunctionType
 ALU = mybir.AluOpType
 
-PAIR = (("y", 2, 0), ("y", 2, 1),)
+PAIR = (("y", 2, 0), ("y", 2, 1), ("a", 1, 0),)
 
 ORDER = """
-TT000 TT001 SI00 SI01 CP TX00 SI02 CSP SI03 XS000 SQ0 XS001 XQ000 TT010 
-TM0 SI10 XQ001 SI11 TT011 MS00 MS01 MQ00 TT100 TX01 SI12 SI13 MQ01 TT101 
-XS010 AM000 AM001 XS011 AM002 XQ010 AS000 TM1 XQ011 SQ1 AS001 TT110 AS002 AM003 
-AM010 AS003 AM011 TT111 AM012 AS010 AS011 AM013 AI00 AS012 YM000 AS013 YM001 YM002 
-TT200 YS000 YS001 YM003 AQ00 YS002 YM010 AI01 YS003 YM011 MS10 YM012 MS11 YI00 
-YS010 TX10 YS011 AQ01 YS012 YM013 YQ00 XS100 MQ10 MQ11 XS101 XQ100 AM100 YS013 
-XQ101 TX11 TT201 AS100 AM101 XS110 YI01 AM102 AM103 XS111 AS101 TX20 XQ110 XQ111 
-AS102 YQ01 AS103 AM110 TT210 AM111 AS110 AM112 ZM000 AS111 AI10 AM113 AS112 ZM010 
-AS113 YM100 TT211 YM101 XS200 XS201 YM102 AQ10 ZM020 YS100 AI11 TX21 YS101 YS102 
-XQ200 XS210 YM103 AQ11 YM110 XS211 XQ201 XQ210 YS103 YM111 XQ211 ZT000 YS110 YM112 
-YI10 YS111 YM113 ZM030 YS112 YM200 YS113 ZT010 YS200 YM201 YQ10 YM202 YI11 YS201 
-YM203 ZM001 YS202 ZT020 YM210 YQ11 YS203 YM211 ZT030 ZM011 YS210 YI20 YM212 YS211 
-ZT001 YM213 YQ20 ZM021 YS212 ZT011 ZM031 YS213 ZT021 ZM100 ZT031 ZM110 YI21 ZM120 
-ZT100 YQ21 ZM130 ZT110 ZT120 ZM101 ZT130 ZM111 ZM121 ZT101 ZT111 ZM131 ZT121 ZM200 
-ZT131 ZM210 ZT200 ZM220 ZM230 ZT210 ZT220 ZM201 ZT230 ZM211 ZT201 ZM221 ZT211 ZM231 
-ZT221 ZT231
+XB XC0 CP XC1 TT000 SI00 SI01 TT001 TM0 SI02 TT010 SI03 MS00 SQ0 
+VT MS01 TT011 VC TX00 SI10 MQ00 SI11 MQ01 TT100 AM000 SI12 AM001 AM002 
+XS000 TT101 XS001 TX01 SI13 XQ000 XQ001 AS000 SQ1 AM003 AS001 CSP AM010 XS010 
+TT110 XS011 TX10 AS010 XQ010 XQ011 AS002 TT111 AS003 YM010 XS100 YM011 AI00 YS010 
+YM012 YS011 YM013 XQ100 YS012 AM011 AQ00 AM012 YS013 TT200 AM013 XS101 TX11 AS011 
+YI01 AS012 AS013 YM000 XQ101 YQ01 XS110 YM001 AI01 XS111 YM002 YS000 TM1 YS001 
+XQ110 AQ01 YS002 YM003 XQ111 MS10 TT201 YM100 MS11 YM110 YS100 MQ10 TX20 MQ11 
+YS110 TT210 YS003 YM111 XS200 YI00 YM112 XS201 YM113 YS111 XQ200 AM110 YS112 XQ201 
+YQ00 AM111 YS113 TT211 ZM000 AS110 AM112 AS111 AM113 YI11 TX21 AS112 AS113 ZT000 
+YM101 XS210 YQ11 YM102 XS211 AI11 YM103 YS101 ZM020 YS102 XQ210 AM100 YS103 AM101 
+AQ11 ZM010 AS100 YI10 AM102 ZM030 AS101 AM103 XQ211 AS102 YQ10 YM200 ZT020 AS103 
+YM201 ZT010 ZM120 YS200 AI10 YM202 YS201 ZT120 YM203 AQ10 ZM130 YS202 ZT030 YM210 
+YS203 ZT130 YM211 ZM111 YS210 YI20 YM212 ZT111 YS211 YM213 YQ20 YS212 ZM011 ZM031 
+ZT011 YS213 ZM001 ZT031 ZM121 YI21 ZM101 ZT001 ZC121 ZM131 YQ21 ZM110 ZT121 ZT101 
+ZM230 ZT131 ZM200 ZT110 ZC230 ZM210 ZT200 ZT230 ZM221 ZT210 ZM231 ZT221 ZM201 ZT231 
+ZM021 ZT201 ZM211 ZT021 ZM220 ZC211 ZM100 ZT220 ZT211 ZT100
 """
 
 
@@ -59,7 +59,8 @@ def tile_coupling_compensated_beams_s11_kernel(
         make_identity(nc, ident_b[:])
 
         xsc = keep.tile([128, M], F32, align_bytes=64)
-        nc.scalar.dma_start(out=xsc[:], in_=x_scale.rearrange("o k -> (o k)").partition_broadcast(128))
+        scale_cols = keep.tile([128, 8], F32, align_bytes=64)
+        nc.sync.dma_start(out=scale_cols[:], in_=x_scale.rearrange("o (p c) -> p (o c)", c=8))
         for v, vec in enumerate((offset, taper)):
             for eg in range(2):
                 row = 8 * v + 4 * eg
@@ -86,29 +87,49 @@ def tile_coupling_compensated_beams_s11_kernel(
         def load_samp(eg):
             nc.sync.dma_start(out=samp_raw[:, :, 512 * eg : 512 * (eg + 1)], in_=samp_rows[:, :, 512 * eg : 512 * (eg + 1)])
 
-        load_x(0, 0)
         for q in range(4):
             nc.sync.dma_start(
                 out=scales_raw[32 * q : 32 * q + 4, :, :].bitcast(I32),
                 in_=cinv_scales[:, 4 * q : 4 * q + 4, :].rearrange("g r n -> r g n").bitcast(I32),
             )
-        load_samp(0)
+        load_x(0, 0)
         nc.sync.dma_start(out=words_raw[:].bitcast(I32), in_=cinv_words.rearrange("g p n -> p g n").bitcast(I32))
+        load_samp(0)
         load_modes(0)
         load_x(0, 1)
-        load_samp(1)
         load_x(1, 0)
-        load_x(1, 1)
+        load_samp(1)
+        load_x(2, 1)
         load_modes(1)
         load_x(2, 0)
-        load_x(2, 1)
         norm_b = keep.tile([128, D], BF16, align_bytes=64)
         nc.sync.dma_start(out=norm_b[:], in_=norm.partition_broadcast(128))
+        load_x(1, 1)
 
-        vec_t = psum.tile([128, 128], BF16, tag="tr", bufs=2)
-        nc.tensor.transpose(vec_t[:], vecs[:], ident_b[:])
         cols = keep.tile([128, 16], F32, align_bytes=64)
-        nc.scalar.copy(cols[:], vec_t[:, 0:16])
+        live = {}
+
+        def XB():
+            for b in range(2):
+                pt = psum.tile([128, 4, 128], F32, tag="tr", bufs=2)
+                for c in range(4):
+                    col = 4 * b + c
+                    nc.tensor.transpose(pt[:, c, :], scale_cols[:, col : col + 1].to_broadcast([128, 128]), ident[:])
+                live["xsc", b] = pt
+
+        def XC(b):
+            nc.scalar.copy(
+                xsc[:].rearrange("p (i c) -> p i c", c=8)[:, :, 4 * b : 4 * b + 4],
+                live["xsc", b][:].rearrange("p c i -> p i c"),
+            )
+
+        def VT():
+            vec_t = psum.tile([128, 128], BF16, tag="tr", bufs=2)
+            nc.tensor.transpose(vec_t[:], vecs[:], ident_b[:])
+            live["vec"] = vec_t
+
+        def VC():
+            nc.scalar.copy(cols[:], live["vec"][:, 0:16])
 
         words = keep.tile([128, 2, 2 * E], U8, align_bytes=64)
         scales = keep.tile([128, 2, E], U8, align_bytes=64)
@@ -148,8 +169,6 @@ def tile_coupling_compensated_beams_s11_kernel(
         sq, sqs = pairs_of("s", 512)
         aq, aqs = pairs_of("a", 512)
         yq, yqs = pairs_of("y", 512)
-        live = {}
-
         def TT(c, h, i):
             if i == 0:
                 xb_new = work.tile([128, 2, M], BF16, tag="xb", bufs=4, align_bytes=64)
@@ -301,13 +320,13 @@ def tile_coupling_compensated_beams_s11_kernel(
         def ZT(c, i, j):
             d0 = 512 * j
             res = work.tile([128, 512], F32, tag="res", bufs=6)
-            engine = nc.gpsimd if (c, i, j) in () else nc.vector
+            engine = nc.gpsimd if (c, i, j) in ((1, 2, 1), (2, 3, 0), (2, 1, 1),) else nc.vector
             engine.tensor_tensor(out=res[:], in0=live["z", c, i, j][:], in1=norm_b[:, d0 : d0 + 512], op=ALU.mult)
             nc.sync.dma_start(out=out_rows[c, :, i, d0 : d0 + 512], in_=res[:])
 
         ops = {
             "TT": TT, "TX": TX, "XS": XS, "XQ": XQ, "TM": TM, "MS": MS, "MQ": MQ, "SI": SI, "SQ": SQ, "AM": AM, "AS": AS,
-            "AI": AI, "AQ": AQ, "YM": YM, "YS": YS, "YI": YI, "YQ": YQ, "ZM": ZM, "ZC": ZC, "ZT": ZT, "CP": CP, "CS": CSP,
+            "AI": AI, "AQ": AQ, "YM": YM, "YS": YS, "YI": YI, "YQ": YQ, "ZM": ZM, "ZC": ZC, "ZT": ZT, "CP": CP, "CS": CSP, "XB": XB, "XC": XC, "VT": VT, "VC": VC,
         }
         for op in ORDER.split():
             ops[op[:2]](*[int(v) for v in op[2:].replace("P", "")])

@@ -17,25 +17,27 @@ FP4X4 = mybir.dt.float4_e2m1fn_x4
 ACT = mybir.ActivationFunctionType
 ALU = mybir.AluOpType
 
-PAIR = (("y", 2, 0), ("y", 2, 1), ("a", 1, 0),)
+PAIR = (("y", 2, 1), ("a", 1, 0), ("y", 2, 0),)
+
+LAST = (2, 3, 0)
 
 ORDER = """
-XB XC0 CP XC1 TT000 SI00 SI01 TT001 TM0 SI02 TT010 SI03 MS00 SQ0 
-VT MS01 TT011 VC TX00 SI10 MQ00 SI11 MQ01 TT100 AM000 SI12 AM001 AM002 
-XS000 TT101 XS001 TX01 SI13 XQ000 XQ001 AS000 SQ1 AM003 AS001 CSP AM010 XS010 
-TT110 XS011 TX10 AS010 XQ010 XQ011 AS002 TT111 AS003 YM010 XS100 YM011 AI00 YS010 
-YM012 YS011 YM013 XQ100 YS012 AM011 AQ00 AM012 YS013 TT200 AM013 XS101 TX11 AS011 
-YI01 AS012 AS013 YM000 XQ101 YQ01 XS110 YM001 AI01 XS111 YM002 YS000 TM1 YS001 
-XQ110 AQ01 YS002 YM003 XQ111 MS10 TT201 YM100 MS11 YM110 YS100 MQ10 TX20 MQ11 
-YS110 TT210 YS003 YM111 XS200 YI00 YM112 XS201 YM113 YS111 XQ200 AM110 YS112 XQ201 
-YQ00 AM111 YS113 TT211 ZM000 AS110 AM112 AS111 AM113 YI11 TX21 AS112 AS113 ZT000 
-YM101 XS210 YQ11 YM102 XS211 AI11 YM103 YS101 ZM020 YS102 XQ210 AM100 YS103 AM101 
-AQ11 ZM010 AS100 YI10 AM102 ZM030 AS101 AM103 XQ211 AS102 YQ10 YM200 ZT020 AS103 
-YM201 ZT010 ZM120 YS200 AI10 YM202 YS201 ZT120 YM203 AQ10 ZM130 YS202 ZT030 YM210 
-YS203 ZT130 YM211 ZM111 YS210 YI20 YM212 ZT111 YS211 YM213 YQ20 YS212 ZM011 ZM031 
-ZT011 YS213 ZM001 ZT031 ZM121 YI21 ZM101 ZT001 ZC121 ZM131 YQ21 ZM110 ZT121 ZT101 
-ZM230 ZT131 ZM200 ZT110 ZC230 ZM210 ZT200 ZT230 ZM221 ZT210 ZM231 ZT221 ZM201 ZT231 
-ZM021 ZT201 ZM211 ZT021 ZM220 ZC211 ZM100 ZT220 ZT211 ZT100
+XB SI00 XC1 XC0 SI01 TT000 TM0 SI02 TT001 SI03 MS00 SQ0 VT MS01 
+TT010 VC TX00 SI10 TT011 SI11 SI12 MQ0 SI13 CP AM000 AM001 XS000 SQ1 
+AM002 XS001 TT110 TX01 AS000 AS001 TT111 AS002 AM003 AM010 XS010 CSP AM011 TT100 
+XS011 TX11 AS003 XQ00 AS010 XQ01 AS011 AM012 AM013 AI00 XS110 YM000 XS111 TT101 
+TM1 AS012 AS013 AQ00 YS000 YM001 AI01 MS10 YM002 YS001 YM003 TT210 YS002 YM010 
+YS003 YM011 AQ01 MS11 YM012 TT211 YS010 TX10 YS011 YI00 YS012 YM013 XS100 MQ1 
+XS101 XQ10 AM100 YS013 AM110 XQ11 TX21 AS110 YQ00 AS100 YI01 YM100 XS210 YM101 
+YS100 TT200 YM102 YS101 YM103 YQ01 YS102 AM111 TT201 AM112 YS103 ZM000 AS111 AM113 
+YI10 AM101 AS112 ZM030 AS113 AM102 ZT000 XS211 AM103 ZM020 YQ10 AS101 TX20 AI11 
+AS102 ZT030 YM110 AS103 AQ11 YM111 XS200 AI10 YM112 XS201 XQ20 ZM010 YS110 XQ21 
+YM113 YS111 AQ10 YM210 YS112 ZT020 ZM021 YS113 ZT010 YM211 YS210 YI11 YM212 YS211 
+YM213 ZT021 YS212 YM200 YQ11 ZM011 YS213 YM201 ZT011 YS200 YM202 YI21 ZM001 YS201 
+YQ21 YM203 ZT001 YS202 ZM111 ZM121 YS203 ZT111 ZM110 ZC121 YI20 ZM130 ZT121 ZT110 
+ZM120 ZC130 ZM131 ZC120 YQ20 ZM031 ZT130 ZT131 ZM220 ZT031 ZM221 ZC220 ZT120 ZM211 
+ZC221 ZM210 ZT211 ZT220 ZM200 ZT210 ZM231 ZT200 ZT221 ZM101 ZC231 ZM201 ZT101 ZT231 
+ZM100 ZT201 ZM230 ZT100 ZT230
 """
 
 
@@ -87,24 +89,24 @@ def tile_coupling_compensated_beams_s11_kernel(
         def load_samp(eg):
             nc.sync.dma_start(out=samp_raw[:, :, 512 * eg : 512 * (eg + 1)], in_=samp_rows[:, :, 512 * eg : 512 * (eg + 1)])
 
+        load_samp(0)
+        load_x(0, 0)
         for q in range(4):
             nc.sync.dma_start(
                 out=scales_raw[32 * q : 32 * q + 4, :, :].bitcast(I32),
                 in_=cinv_scales[:, 4 * q : 4 * q + 4, :].rearrange("g r n -> r g n").bitcast(I32),
             )
-        load_x(0, 0)
-        nc.sync.dma_start(out=words_raw[:].bitcast(I32), in_=cinv_words.rearrange("g p n -> p g n").bitcast(I32))
-        load_samp(0)
         load_modes(0)
-        load_x(0, 1)
-        load_x(1, 0)
         load_samp(1)
+        load_x(0, 1)
         load_x(2, 1)
+        nc.sync.dma_start(out=words_raw[:].bitcast(I32), in_=cinv_words.rearrange("g p n -> p g n").bitcast(I32))
+        load_x(1, 1)
         load_modes(1)
-        load_x(2, 0)
         norm_b = keep.tile([128, D], BF16, align_bytes=64)
         nc.sync.dma_start(out=norm_b[:], in_=norm.partition_broadcast(128))
-        load_x(1, 1)
+        load_x(1, 0)
+        load_x(2, 0)
 
         cols = keep.tile([128, 16], F32, align_bytes=64)
         live = {}
@@ -118,10 +120,12 @@ def tile_coupling_compensated_beams_s11_kernel(
                 live["xsc", b] = pt
 
         def XC(b):
-            nc.scalar.copy(
-                xsc[:].rearrange("p (i c) -> p i c", c=8)[:, :, 4 * b : 4 * b + 4],
-                live["xsc", b][:].rearrange("p c i -> p i c"),
-            )
+            dst = xsc[:].rearrange("p (i c) -> p i c", c=8)[:, :, 4 * b : 4 * b + 4]
+            src = live["xsc", b][:].rearrange("p c i -> p i c")
+            if b == 0:
+                nc.scalar.copy(dst, src)
+            else:
+                nc.vector.tensor_copy(out=dst, in_=src)
 
         def VT():
             vec_t = psum.tile([128, 128], BF16, tag="tr", bufs=2)
@@ -135,15 +139,10 @@ def tile_coupling_compensated_beams_s11_kernel(
         scales = keep.tile([128, 2, E], U8, align_bytes=64)
 
         def permute(dst, src, w):
-            n = 64 * w
-            for g in range(2):
-                for eg in range(2):
-                    d32 = dst[:, g, :].bitcast(I32)[:, n * eg : n * (eg + 1)]
-                    s32 = src[:, g, :].bitcast(I32)[:, n * eg : n * (eg + 1)]
-                    nc.vector.tensor_copy(
-                        out=d32.rearrange("p (t q w) -> p t q w", t=4, w=w),
-                        in_=s32.rearrange("p (q t w) -> p t q w", t=4, w=w),
-                    )
+            nc.vector.tensor_copy(
+                out=dst[:].rearrange("p g n -> p (g n)").bitcast(I32).rearrange("p (a t q w) -> p a t q w", a=4, t=4, w=w),
+                in_=src[:].rearrange("p g n -> p (g n)").bitcast(I32).rearrange("p (a q t w) -> p a t q w", a=4, t=4, w=w),
+            )
 
         def CP():
             permute(words, words_raw, 4)
@@ -170,7 +169,7 @@ def tile_coupling_compensated_beams_s11_kernel(
         aq, aqs = pairs_of("a", 512)
         yq, yqs = pairs_of("y", 512)
         def TT(c, h, i):
-            if i == 0:
+            if ("xb", c, h) not in live:
                 xb_new = work.tile([128, 2, M], BF16, tag="xb", bufs=4, align_bytes=64)
                 live["xb", c, h] = xb_new
             nc.vector.tensor_tensor(
@@ -184,14 +183,16 @@ def tile_coupling_compensated_beams_s11_kernel(
                     nc.tensor.transpose(pt[:, i, u, :], w[i][:, k0 + u : k0 + 256 : 2], ident[:])
             live[key] = pt
 
-        def lift(key):
+        def lift(key, operand, part):
             pt = live[key]
-            xi = work.tile([128, 256, 4], BF16, tag="xi", bufs=4, align_bytes=64)
+            if operand not in live:
+                xi_new = work.tile([128, 512, 4], BF16, tag="xi", bufs=6, align_bytes=64)
+                live[operand] = xi_new
+            half = live[operand][:, 256 * part : 256 * (part + 1), :]
             nc.scalar.copy(
-                xi[:].rearrange("p n t -> p (n t)").bitcast(F32).rearrange("p (i r u) -> p i r u", i=2, u=2),
+                half.rearrange("p n t -> p (n t)").bitcast(F32).rearrange("p (i r u) -> p i r u", i=2, u=2),
                 pt[:].rearrange("p i u r -> p i r u"),
             )
-            live[key] = xi
 
         def quant(src, codes, planes):
             nc.vector.quantize_mx(out=codes.bitcast(FP8X4), scales=planes, in_=src)
@@ -202,25 +203,23 @@ def tile_coupling_compensated_beams_s11_kernel(
                 flip(("x", c, h, g), [xb[:, i, :].bitcast(F32) for i in range(2)], 256 * g)
 
         def XS(c, h, g):
-            lift(("x", c, h, g))
+            lift(("x", c, h, g), ("xi", c, g), h)
 
-        def XQ(c, h, g):
-            s = slice(256 * h, 256 * (h + 1))
-            quant(live["x", c, h, g][:].rearrange("p n t -> p (n t)"), xq[c, g][:, s], xqs[c, g][:, s])
+        def XQ(c, g):
+            quant(live["xi", c, g][:].rearrange("p n t -> p (n t)"), xq[c, g][:], xqs[c, g][:])
 
         def TM(j):
             for b in range(2):
                 flip(("m", j, b), [modes_raw[j][:, 2 * b + i, :].bitcast(F32) for i in range(2)], 0)
 
         def MS(j, b):
-            lift(("m", j, b))
+            lift(("m", j, b), ("mi", j), b)
 
-        def MQ(j, b):
-            s = slice(256 * b, 256 * (b + 1))
-            quant(live["m", j, b][:].rearrange("p n t -> p (n t)"), mq[j,][:, s], mqs[j,][:, s])
+        def MQ(j):
+            quant(live["mi", j][:].rearrange("p n t -> p (n t)"), mq[j,][:], mqs[j,][:])
 
         def SI(eg, t):
-            if t == 0:
+            if ("s", eg) not in live:
                 si_new = work.tile([128, 512, 4], BF16, tag="si", bufs=2, align_bytes=64)
                 live["s", eg] = si_new
             src = samp_raw[:, :, 512 * eg : 512 * (eg + 1)].rearrange("p j (q t r) -> p t q r j", t=4, r=8)
@@ -253,7 +252,7 @@ def tile_coupling_compensated_beams_s11_kernel(
 
         def empty(kind, i, eg, t):
             key = kind + "raw", i, eg
-            if t == 0:
+            if key not in live:
                 raw_new = work.tile([128, 2048], BF16, tag="raw", bufs=4, align_bytes=64)
                 live[key] = raw_new
             raw = live[key]
@@ -284,7 +283,7 @@ def tile_coupling_compensated_beams_s11_kernel(
                 )
             else:
                 nc.vector.tensor_copy(
-                    out=lay[:].rearrange("p (n t) -> p n t", t=4), in_=raw[:].rearrange("p (t n) -> p n t", t=4)
+                    out=lay[:].rearrange("p (c i t) -> p c t i", i=4, t=4), in_=raw[:].rearrange("p (t c i) -> p c t i", t=4, i=4)
                 )
             live[kind + "lay", i, eg] = lay
 
@@ -320,7 +319,13 @@ def tile_coupling_compensated_beams_s11_kernel(
         def ZT(c, i, j):
             d0 = 512 * j
             res = work.tile([128, 512], F32, tag="res", bufs=6)
-            engine = nc.gpsimd if (c, i, j) in ((1, 2, 1), (2, 3, 0), (2, 1, 1),) else nc.vector
+            if (c, i, j) == LAST:
+                for n in (slice(0, 256), slice(256, 512)):
+                    dn = slice(d0 + n.start, d0 + n.stop)
+                    nc.vector.tensor_tensor(out=res[:, n], in0=live["z", c, i, j][:, n], in1=norm_b[:, dn], op=ALU.mult)
+                    nc.sync.dma_start(out=out_rows[c, :, i, dn], in_=res[:, n])
+                return
+            engine = nc.gpsimd if (c, i, j) in ((1, 2, 0), (1, 2, 1), (1, 3, 0), (2, 2, 1), (2, 3, 1), (2, 2, 0),) else nc.vector
             engine.tensor_tensor(out=res[:], in0=live["z", c, i, j][:], in1=norm_b[:, d0 : d0 + 512], op=ALU.mult)
             nc.sync.dma_start(out=out_rows[c, :, i, d0 : d0 + 512], in_=res[:])
 

@@ -17,27 +17,27 @@ FP4X4 = mybir.dt.float4_e2m1fn_x4
 ACT = mybir.ActivationFunctionType
 ALU = mybir.AluOpType
 
-PAIR = (("y", 2, 1), ("a", 1, 0), ("y", 2, 0),)
+PAIR = (("y", 1, 0), ("y", 2, 0),)
 
-LAST = (2, 3, 0)
+LAST = (1, 3, 1)
 
 ORDER = """
-XB SI00 XC1 XC0 SI01 TT000 TM0 SI02 TT001 SI03 MS00 SQ0 VT MS01 
-TT010 VC TX00 SI10 TT011 SI11 SI12 MQ0 SI13 CP AM000 AM001 XS000 SQ1 
-AM002 XS001 TT110 TX01 AS000 AS001 TT111 AS002 AM003 AM010 XS010 CSP AM011 TT100 
-XS011 TX11 AS003 XQ00 AS010 XQ01 AS011 AM012 AM013 AI00 XS110 YM000 XS111 TT101 
-TM1 AS012 AS013 AQ00 YS000 YM001 AI01 MS10 YM002 YS001 YM003 TT210 YS002 YM010 
-YS003 YM011 AQ01 MS11 YM012 TT211 YS010 TX10 YS011 YI00 YS012 YM013 XS100 MQ1 
-XS101 XQ10 AM100 YS013 AM110 XQ11 TX21 AS110 YQ00 AS100 YI01 YM100 XS210 YM101 
-YS100 TT200 YM102 YS101 YM103 YQ01 YS102 AM111 TT201 AM112 YS103 ZM000 AS111 AM113 
-YI10 AM101 AS112 ZM030 AS113 AM102 ZT000 XS211 AM103 ZM020 YQ10 AS101 TX20 AI11 
-AS102 ZT030 YM110 AS103 AQ11 YM111 XS200 AI10 YM112 XS201 XQ20 ZM010 YS110 XQ21 
-YM113 YS111 AQ10 YM210 YS112 ZT020 ZM021 YS113 ZT010 YM211 YS210 YI11 YM212 YS211 
-YM213 ZT021 YS212 YM200 YQ11 ZM011 YS213 YM201 ZT011 YS200 YM202 YI21 ZM001 YS201 
-YQ21 YM203 ZT001 YS202 ZM111 ZM121 YS203 ZT111 ZM110 ZC121 YI20 ZM130 ZT121 ZT110 
-ZM120 ZC130 ZM131 ZC120 YQ20 ZM031 ZT130 ZT131 ZM220 ZT031 ZM221 ZC220 ZT120 ZM211 
-ZC221 ZM210 ZT211 ZT220 ZM200 ZT210 ZM231 ZT200 ZT221 ZM101 ZC231 ZM201 ZT101 ZT231 
-ZM100 ZT201 ZM230 ZT100 ZT230
+XB SI00 XC1 XC0 SI01 TT000 SI02 TM0 TT001 SI03 MS00 SQ0 MS01 CP 
+TX00 MQ0 SI10 TT010 SI11 AM000 SI12 AM001 AM002 TT011 SI13 XS000 TT100 VT 
+XS001 VC SQ1 TX01 AS000 TT101 AS001 AS002 AM010 TT110 AM011 XS010 AM012 XS011 
+CSP TX10 AS010 XQ00 AS011 XQ01 AS012 TT111 AM013 YM010 XS100 YM011 XS101 TT210 
+TX11 YS010 TT211 YS011 AS013 YM012 TT200 XS110 YM013 YS012 AM003 XQ10 YM000 YS013 
+AI01 YM001 XS111 AS003 TX21 YI01 YS000 YS001 YM002 XQ11 XS210 YM003 YQ01 XS211 
+YM110 AQ01 YS002 TM1 AI00 YS110 YS003 YM111 TT201 MS10 YM112 YS111 YM113 AQ00 
+YS112 YM100 YI00 YS113 YM101 MS11 YM102 YI11 YS100 TX20 YS101 YQ00 YQ11 YM103 
+YS102 MQ1 ZM010 XS200 ZM000 ZT010 XS201 AM100 XQ20 AM101 YS103 ZM020 XQ21 AS100 
+AM102 YI10 ZM030 AS101 ZT000 AM103 AS102 YM210 YQ10 AS103 YM211 ZT020 YS210 YM212 
+AI10 YS211 YM213 YS212 AM110 ZT030 ZM130 YS213 AQ10 AM111 AS110 AM112 YI21 ZM110 
+AS111 AM113 AS112 YM200 ZT130 AS113 YM201 YQ21 YS200 YM202 ZT110 ZM120 AI11 YS201 
+YM203 YS202 ZM100 ZT120 AQ11 YS203 ZT100 ZM001 YI20 ZM031 ZT001 ZM011 YQ20 ZM101 
+ZT031 ZM200 ZT011 ZM210 ZT101 ZM021 ZT200 ZC210 ZM221 ZT021 ZT210 ZM231 ZC221 ZM211 
+ZT231 ZT221 ZM220 ZC211 ZM121 ZT220 ZT211 ZM111 ZT121 ZM230 ZT111 ZM201 ZT230 ZM131 
+ZT201 ZT131
 """
 
 
@@ -53,7 +53,7 @@ def tile_coupling_compensated_beams_s11_kernel(
 
         scales_raw = keep.tile([128, 2, E], U8, align_bytes=64)
         nc.vector.memset(scales_raw[:].bitcast(I32), 0)
-        vecs = keep.tile([128, 128], BF16, align_bytes=64)
+        vecs = keep.tile([128, 256], BF16, align_bytes=64)
         nc.gpsimd.memset(vecs[:], 0.0)
         ident = keep.tile([128, 128], F32, align_bytes=64)
         make_identity(nc, ident[:])
@@ -63,13 +63,6 @@ def tile_coupling_compensated_beams_s11_kernel(
         xsc = keep.tile([128, M], F32, align_bytes=64)
         scale_cols = keep.tile([128, 8], F32, align_bytes=64)
         nc.sync.dma_start(out=scale_cols[:], in_=x_scale.rearrange("o (p c) -> p (o c)", c=8))
-        for v, vec in enumerate((offset, taper)):
-            for eg in range(2):
-                row = 8 * v + 4 * eg
-                nc.scalar.dma_start(
-                    out=vecs[row : row + 4, :].rearrange("t (q r) -> t q r", r=8),
-                    in_=vec[512 * eg : 512 * (eg + 1)].rearrange("(q t r) -> t q r", t=4, r=8),
-                )
         x_rows = x_bytes.rearrange("(c p i) k -> c p i k", p=128, i=4)
         x_raw = {}
 
@@ -91,22 +84,27 @@ def tile_coupling_compensated_beams_s11_kernel(
 
         load_samp(0)
         load_x(0, 0)
+        load_modes(0)
+        nc.sync.dma_start(out=words_raw[:].bitcast(I32), in_=cinv_words.rearrange("g p n -> p g n").bitcast(I32))
+        load_samp(1)
+        load_x(0, 1)
+        for v, vec in enumerate((offset, taper)):
+            nc.sync.dma_start(
+                out=vecs[4 * v : 4 * v + 4, :].rearrange("t (a r) -> t a r", r=8),
+                in_=vec.rearrange("(a t r) -> t a r", t=4, r=8),
+            )
         for q in range(4):
             nc.sync.dma_start(
                 out=scales_raw[32 * q : 32 * q + 4, :, :].bitcast(I32),
                 in_=cinv_scales[:, 4 * q : 4 * q + 4, :].rearrange("g r n -> r g n").bitcast(I32),
             )
-        load_modes(0)
-        load_samp(1)
-        load_x(0, 1)
-        load_x(2, 1)
-        nc.sync.dma_start(out=words_raw[:].bitcast(I32), in_=cinv_words.rearrange("g p n -> p g n").bitcast(I32))
+        load_x(1, 0)
         load_x(1, 1)
+        load_x(2, 1)
+        load_x(2, 0)
         load_modes(1)
         norm_b = keep.tile([128, D], BF16, align_bytes=64)
         nc.sync.dma_start(out=norm_b[:], in_=norm.partition_broadcast(128))
-        load_x(1, 0)
-        load_x(2, 0)
 
         cols = keep.tile([128, 16], F32, align_bytes=64)
         live = {}
@@ -128,12 +126,13 @@ def tile_coupling_compensated_beams_s11_kernel(
                 nc.vector.tensor_copy(out=dst, in_=src)
 
         def VT():
-            vec_t = psum.tile([128, 128], BF16, tag="tr", bufs=2)
-            nc.tensor.transpose(vec_t[:], vecs[:], ident_b[:])
+            vec_t = psum.tile([128, 2, 128], BF16, tag="tr", bufs=2)
+            for eg in range(2):
+                nc.tensor.transpose(vec_t[:, eg, :], vecs[:, 128 * eg : 128 * (eg + 1)], ident_b[:])
             live["vec"] = vec_t
 
         def VC():
-            nc.scalar.copy(cols[:], live["vec"][:, 0:16])
+            nc.scalar.copy(cols[:].rearrange("p (g t) -> p g t", g=2), live["vec"][:, :, 0:8])
 
         words = keep.tile([128, 2, 2 * E], U8, align_bytes=64)
         scales = keep.tile([128, 2, E], U8, align_bytes=64)
@@ -261,11 +260,11 @@ def tile_coupling_compensated_beams_s11_kernel(
             else:
                 dst = raw[:, 512 * t : 512 * (t + 1)]
             acc = live[kind, i, eg, t]
-            col = 4 * eg + t
+            col = 8 * eg + t
             if kind == "y":
                 nc.scalar.activation(out=dst, in_=acc[:], func=ACT.Identity, bias=cols[:, col : col + 1], scale=1.0)
             else:
-                nc.scalar.activation(out=dst, in_=acc[:], func=ACT.Copy, scale=cols[:, 8 + col : 9 + col])
+                nc.scalar.activation(out=dst, in_=acc[:], func=ACT.Copy, scale=cols[:, col + 4 : col + 5])
 
         def AS(j, eg, t):
             empty("a", j, eg, t)
@@ -325,7 +324,7 @@ def tile_coupling_compensated_beams_s11_kernel(
                     nc.vector.tensor_tensor(out=res[:, n], in0=live["z", c, i, j][:, n], in1=norm_b[:, dn], op=ALU.mult)
                     nc.sync.dma_start(out=out_rows[c, :, i, dn], in_=res[:, n])
                 return
-            engine = nc.gpsimd if (c, i, j) in ((1, 2, 0), (1, 2, 1), (1, 3, 0), (2, 2, 1), (2, 3, 1), (2, 2, 0),) else nc.vector
+            engine = nc.gpsimd if (c, i, j) in ((2, 1, 0), (2, 1, 1), (2, 2, 1),) else nc.vector
             engine.tensor_tensor(out=res[:], in0=live["z", c, i, j][:], in1=norm_b[:, d0 : d0 + 512], op=ALU.mult)
             nc.sync.dma_start(out=out_rows[c, :, i, d0 : d0 + 512], in_=res[:])
 

@@ -17,28 +17,13 @@ FP4X4 = mybir.dt.float4_e2m1fn_x4
 ACT = mybir.ActivationFunctionType
 ALU = mybir.AluOpType
 
-PAIR = (("y", 1, 0), ("y", 2, 0),)
-
-LAST = (1, 3, 1)
-
-ORDER = """
-XB SI00 XC1 XC0 SI01 TT000 SI02 TM0 TT001 SI03 MS00 SQ0 MS01 CP 
-TX00 MQ0 SI10 TT010 SI11 AM000 SI12 AM001 AM002 TT011 SI13 XS000 TT100 VT 
-XS001 VC SQ1 TX01 AS000 TT101 AS001 AS002 AM010 TT110 AM011 XS010 AM012 XS011 
-CSP TX10 AS010 XQ00 AS011 XQ01 AS012 TT111 AM013 YM010 XS100 YM011 XS101 TT210 
-TX11 YS010 TT211 YS011 AS013 YM012 TT200 XS110 YM013 YS012 AM003 XQ10 YM000 YS013 
-AI01 YM001 XS111 AS003 TX21 YI01 YS000 YS001 YM002 XQ11 XS210 YM003 YQ01 XS211 
-YM110 AQ01 YS002 TM1 AI00 YS110 YS003 YM111 TT201 MS10 YM112 YS111 YM113 AQ00 
-YS112 YM100 YI00 YS113 YM101 MS11 YM102 YI11 YS100 TX20 YS101 YQ00 YQ11 YM103 
-YS102 MQ1 ZM010 XS200 ZM000 ZT010 XS201 AM100 XQ20 AM101 YS103 ZM020 XQ21 AS100 
-AM102 YI10 ZM030 AS101 ZT000 AM103 AS102 YM210 YQ10 AS103 YM211 ZT020 YS210 YM212 
-AI10 YS211 YM213 YS212 AM110 ZT030 ZM130 YS213 AQ10 AM111 AS110 AM112 YI21 ZM110 
-AS111 AM113 AS112 YM200 ZT130 AS113 YM201 YQ21 YS200 YM202 ZT110 ZM120 AI11 YS201 
-YM203 YS202 ZM100 ZT120 AQ11 YS203 ZT100 ZM001 YI20 ZM031 ZT001 ZM011 YQ20 ZM101 
-ZT031 ZM200 ZT011 ZM210 ZT101 ZM021 ZT200 ZC210 ZM221 ZT021 ZT210 ZM231 ZC221 ZM211 
-ZT231 ZT221 ZM220 ZC211 ZM121 ZT220 ZT211 ZM111 ZT121 ZM230 ZT111 ZM201 ZT230 ZM131 
-ZT201 ZT131
-"""
+CHUNKS = 3
+BANKS = 8
+PAIRS_FIRST = (("y", 2, 1),)
+SHARED = ((1, 0, 0), (1, 1, 0), (0, 3, 1), (1, 2, 1))
+LAST = (2, 3, 1)
+BUFS = {"xb": 6, "operand": 10, "raw": 5, "operand_ya": 5, "copied": 4, "result": 6}
+TURN = {"vector": 3, "scalar": 3, "gpsimd": 1, "tensor": 2}
 
 
 def tile_coupling_compensated_beams_s11_kernel(
@@ -48,94 +33,120 @@ def tile_coupling_compensated_beams_s11_kernel(
     with ExitStack() as ctx:
         ctx.enter_context(tc.manual_schedule())
         keep = ctx.enter_context(tc.tile_pool(name="keep", bufs=1))
-        work = ctx.enter_context(tc.tile_pool(name="work", bufs=3))
-        psum = ctx.enter_context(tc.psum_pool(name="psum", bufs=2))
+        work = ctx.enter_context(tc.tile_pool(name="work", bufs=1))
+        psum = ctx.enter_context(tc.psum_pool(name="psum", bufs=1))
 
+        ident = keep.tile([128, 128], F32, align_bytes=64)
+        make_identity(nc, ident[:])
         scales_raw = keep.tile([128, 2, E], U8, align_bytes=64)
         nc.vector.memset(scales_raw[:].bitcast(I32), 0)
         vecs = keep.tile([128, 256], BF16, align_bytes=64)
         nc.gpsimd.memset(vecs[:], 0.0)
-        ident = keep.tile([128, 128], F32, align_bytes=64)
-        make_identity(nc, ident[:])
         ident_b = keep.tile([128, 128], BF16, align_bytes=64)
         make_identity(nc, ident_b[:])
 
-        xsc = keep.tile([128, M], F32, align_bytes=64)
         scale_cols = keep.tile([128, 8], F32, align_bytes=64)
-        nc.sync.dma_start(out=scale_cols[:], in_=x_scale.rearrange("o (p c) -> p (o c)", c=8))
-        x_rows = x_bytes.rearrange("(c p i) k -> c p i k", p=128, i=4)
-        x_raw = {}
-
-        def load_x(c, h):
-            x_in = keep.tile([128, 2, M], U8, name=f"x_raw_{c}{h}", align_bytes=64)
-            nc.sync.dma_start(out=x_in[:], in_=x_rows[c, :, 2 * h : 2 * h + 2, :])
-            x_raw[c, h] = x_in
-
-        words_raw = keep.tile([128, 2, 2 * E], U8, align_bytes=64)
         samp_raw = keep.tile([128, 4, E], BF16, align_bytes=64)
-        samp_rows = samp.rearrange("(p j) e -> p j e", j=4)
+        words_raw = keep.tile([128, 2, 2 * E], U8, align_bytes=64)
+        norm_b = keep.tile([128, D], BF16, align_bytes=64)
         modes_raw = [keep.tile([128, 4, P], BF16, name=f"modes_raw_{j}", align_bytes=64) for j in range(2)]
+        x_row = {}
 
-        def load_modes(j):
-            nc.sync.dma_start(out=modes_raw[j][:], in_=modes[512 * j : 512 * (j + 1), :].rearrange("(i p) k -> p i k", p=128))
+        def load_x(c, first, count):
+            x_raw = keep.tile([128, count, M], U8, name=f"x_raw_{c}_{first}", align_bytes=64)
+            rows = x_bytes.rearrange("(c p i) k -> c p i k", p=128, i=4)
+            nc.sync.dma_start(out=x_raw[:], in_=rows[c, :, first : first + count, :])
+            for n in range(count):
+                x_row[c, first + n] = x_raw[:, n, :]
 
         def load_samp(eg):
-            nc.sync.dma_start(out=samp_raw[:, :, 512 * eg : 512 * (eg + 1)], in_=samp_rows[:, :, 512 * eg : 512 * (eg + 1)])
+            cols = slice(512 * eg, 512 * (eg + 1))
+            nc.sync.dma_start(out=samp_raw[:, :, cols], in_=samp.rearrange("(p j) e -> p j e", j=4)[:, :, cols])
 
+        def load_modes(j):
+            rows = modes[512 * j : 512 * (j + 1), :]
+            nc.sync.dma_start(out=modes_raw[j][:], in_=rows.rearrange("(p i) k -> p i k", i=4))
+
+        nc.sync.dma_start(out=scale_cols[:], in_=x_scale.rearrange("o (p c) -> p (o c)", c=8))
         load_samp(0)
-        load_x(0, 0)
+        load_x(0, 0, 2)
         load_modes(0)
-        nc.sync.dma_start(out=words_raw[:].bitcast(I32), in_=cinv_words.rearrange("g p n -> p g n").bitcast(I32))
+        load_x(0, 2, 2)
         load_samp(1)
-        load_x(0, 1)
-        for v, vec in enumerate((offset, taper)):
+        for n, vec in enumerate((offset, taper)):
             nc.sync.dma_start(
-                out=vecs[4 * v : 4 * v + 4, :].rearrange("t (a r) -> t a r", r=8),
+                out=vecs[4 * n : 4 * n + 4, :].rearrange("t (a r) -> t a r", r=8),
                 in_=vec.rearrange("(a t r) -> t a r", t=4, r=8),
             )
-        for q in range(4):
+        load_x(1, 0, 4)
+        for n in range(4):
             nc.sync.dma_start(
-                out=scales_raw[32 * q : 32 * q + 4, :, :].bitcast(I32),
-                in_=cinv_scales[:, 4 * q : 4 * q + 4, :].rearrange("g r n -> r g n").bitcast(I32),
+                out=scales_raw[32 * n : 32 * n + 4, :, :].bitcast(I32),
+                in_=cinv_scales[:, 4 * n : 4 * n + 4, :].rearrange("g r n -> r g n").bitcast(I32),
             )
-        load_x(1, 0)
-        load_x(1, 1)
-        load_x(2, 1)
-        load_x(2, 0)
         load_modes(1)
-        norm_b = keep.tile([128, D], BF16, align_bytes=64)
+        nc.sync.dma_start(out=words_raw[:].bitcast(I32), in_=cinv_words.rearrange("g p n -> p g n").bitcast(I32))
+        load_x(2, 0, 4)
         nc.sync.dma_start(out=norm_b[:], in_=norm.partition_broadcast(128))
 
-        cols = keep.tile([128, 16], F32, align_bytes=64)
+        xsc = keep.tile([128, M], F32, align_bytes=64)
+        vec_cols = keep.tile([128, 2, 8], F32, align_bytes=64)
+        words = keep.tile([128, 2, 2 * E], U8, align_bytes=64)
+        scales = keep.tile([128, 2, E], U8, align_bytes=64)
+        codes = {}
+        planes = {}
+        keys = [("x", c, g) for c in range(CHUNKS) for g in range(2)] + [("modes", j) for j in range(2)]
+        keys += [("samp", eg) for eg in range(2)] + [("a", j, eg) for j in range(2) for eg in range(2)]
+        keys += [("y", c, eg) for c in range(CHUNKS) for eg in range(2)]
+        for n, key in enumerate(keys):
+            codes[key] = keep.tile([128, 512], U32, name=f"codes_{n}", align_bytes=64)
+            planes[key] = keep.tile([128, 512], U8, name=f"planes_{n}", align_bytes=64)
+
+        free_banks = list(range(BANKS))
+        bank_of = {}
         live = {}
 
-        def XB():
-            for b in range(2):
-                pt = psum.tile([128, 4, 128], F32, tag="tr", bufs=2)
-                for c in range(4):
-                    col = 4 * b + c
-                    nc.tensor.transpose(pt[:, c, :], scale_cols[:, col : col + 1].to_broadcast([128, 128]), ident[:])
-                live["xsc", b] = pt
+        def take_bank(key, shape, dtype):
+            b = free_banks[0]
+            free_banks.remove(b)
+            bank = psum.tile(shape, dtype, name=f"bank_{b}", tag=f"bank_{b}", bufs=1)
+            bank_of[key] = b
+            live[key] = bank
+            return bank
 
-        def XC(b):
-            dst = xsc[:].rearrange("p (i c) -> p i c", c=8)[:, :, 4 * b : 4 * b + 4]
-            src = live["xsc", b][:].rearrange("p c i -> p i c")
+        def give_bank(key):
+            free_banks.extend([bank_of[key]])
+
+        def work_tile(key, shape, dtype, tag):
+            if key not in live:
+                made = work.tile(shape, dtype, name=tag, tag=tag, bufs=BUFS[tag], align_bytes=64)
+                live[key] = made
+            return live[key]
+
+        def spread_scales():
+            for b in range(2):
+                bank = take_bank(("xsc", b), [128, 4, 128], F32)
+                for n in range(4):
+                    col = scale_cols[:, 4 * b + n : 4 * b + n + 1]
+                    nc.tensor.transpose(bank[:, n, :], col.to_broadcast([128, 128]), ident[:])
+
+        def spread_out(b):
+            dst = xsc[:].rearrange("p (k c) -> p k c", c=8)[:, :, 4 * b : 4 * b + 4]
+            src = live["xsc", b][:].rearrange("p c k -> p k c")
             if b == 0:
                 nc.scalar.copy(dst, src)
             else:
                 nc.vector.tensor_copy(out=dst, in_=src)
+            give_bank(("xsc", b))
 
-        def VT():
-            vec_t = psum.tile([128, 2, 128], BF16, tag="tr", bufs=2)
+        def turn_vecs():
+            bank = take_bank("vecs", [128, 2, 128], BF16)
             for eg in range(2):
-                nc.tensor.transpose(vec_t[:, eg, :], vecs[:, 128 * eg : 128 * (eg + 1)], ident_b[:])
-            live["vec"] = vec_t
+                nc.tensor.transpose(bank[:, eg, :], vecs[:, 128 * eg : 128 * (eg + 1)], ident_b[:])
 
-        def VC():
-            nc.scalar.copy(cols[:].rearrange("p (g t) -> p g t", g=2), live["vec"][:, :, 0:8])
-
-        words = keep.tile([128, 2, 2 * E], U8, align_bytes=64)
-        scales = keep.tile([128, 2, E], U8, align_bytes=64)
+        def vecs_out():
+            nc.scalar.copy(vec_cols[:], live["vecs"][:, :, 0:8])
+            give_bank("vecs")
 
         def permute(dst, src, w):
             nc.vector.tensor_copy(
@@ -143,194 +154,261 @@ def tile_coupling_compensated_beams_s11_kernel(
                 in_=src[:].rearrange("p g n -> p (g n)").bitcast(I32).rearrange("p (a q t w) -> p a t q w", a=4, t=4, w=w),
             )
 
-        def CP():
+        def permute_words():
             permute(words, words_raw, 4)
 
-        def CSP():
+        def permute_scales():
             permute(scales, scales_raw, 2)
 
-        def pairs_of(names, width):
-            return (
-                {k: keep.tile([128, width], U32, name=f"{names}_codes_{'_'.join(str(i) for i in k)}", align_bytes=64) for k in KEYS[names]},
-                {k: keep.tile([128, width], U8, name=f"{names}_scales_{'_'.join(str(i) for i in k)}", align_bytes=64) for k in KEYS[names]},
-            )
+        def widen(c, i):
+            xb = work_tile(("xb", c, i // 2), [128, 2, M], BF16, "xb")
+            nc.vector.tensor_tensor(out=xb[:, i % 2, :], in0=x_row[c, i].bitcast(FP8), in1=xsc[:], op=ALU.mult)
 
-        KEYS = {
-            "x": [(c, g) for c in range(3) for g in range(2)],
-            "m": [(j,) for j in range(2)],
-            "s": [(eg,) for eg in range(2)],
-            "a": [(j, eg) for j in range(2) for eg in range(2)],
-            "y": [(c, eg) for c in range(3) for eg in range(2)],
-        }
-        xq, xqs = pairs_of("x", 512)
-        mq, mqs = pairs_of("m", 512)
-        sq, sqs = pairs_of("s", 512)
-        aq, aqs = pairs_of("a", 512)
-        yq, yqs = pairs_of("y", 512)
-        def TT(c, h, i):
-            if ("xb", c, h) not in live:
-                xb_new = work.tile([128, 2, M], BF16, tag="xb", bufs=4, align_bytes=64)
-                live["xb", c, h] = xb_new
-            nc.vector.tensor_tensor(
-                out=live["xb", c, h][:, i, :], in0=x_raw[c, h][:, i, :].bitcast(FP8), in1=xsc[:], op=ALU.mult
-            )
-
-        def flip(key, w, k0):
-            pt = psum.tile([128, 2, 2, 128], F32, tag="tr", bufs=2)
-            for i in range(2):
+        def turn(key, rows, k0):
+            bank = take_bank(key, [128, 2, 2, 128], F32)
+            for n in range(2):
+                row_words = rows[n].bitcast(F32)
                 for u in range(2):
-                    nc.tensor.transpose(pt[:, i, u, :], w[i][:, k0 + u : k0 + 256 : 2], ident[:])
-            live[key] = pt
+                    nc.tensor.transpose(bank[:, n, u, :], row_words[:, k0 + u : k0 + 256 : 2], ident[:])
 
-        def lift(key, operand, part):
-            pt = live[key]
-            if operand not in live:
-                xi_new = work.tile([128, 512, 4], BF16, tag="xi", bufs=6, align_bytes=64)
-                live[operand] = xi_new
-            half = live[operand][:, 256 * part : 256 * (part + 1), :]
-            nc.scalar.copy(
-                half.rearrange("p n t -> p (n t)").bitcast(F32).rearrange("p (i r u) -> p i r u", i=2, u=2),
-                pt[:].rearrange("p i u r -> p i r u"),
-            )
-
-        def quant(src, codes, planes):
-            nc.vector.quantize_mx(out=codes.bitcast(FP8X4), scales=planes, in_=src)
-
-        def TX(c, h):
+        def turn_x(c, h):
             xb = live["xb", c, h]
             for g in range(2):
-                flip(("x", c, h, g), [xb[:, i, :].bitcast(F32) for i in range(2)], 256 * g)
+                turn(("xt", c, h, g), [xb[:, n, :] for n in range(2)], 256 * g)
 
-        def XS(c, h, g):
-            lift(("x", c, h, g), ("xi", c, g), h)
+        def turn_modes(j):
+            for h in range(2):
+                turn(("mt", j, h), [modes_raw[j][:, 2 * h + n, :] for n in range(2)], 0)
 
-        def XQ(c, g):
-            quant(live["xi", c, g][:].rearrange("p n t -> p (n t)"), xq[c, g][:], xqs[c, g][:])
-
-        def TM(j):
-            for b in range(2):
-                flip(("m", j, b), [modes_raw[j][:, 2 * b + i, :].bitcast(F32) for i in range(2)], 0)
-
-        def MS(j, b):
-            lift(("m", j, b), ("mi", j), b)
-
-        def MQ(j):
-            quant(live["mi", j][:].rearrange("p n t -> p (n t)"), mq[j,][:], mqs[j,][:])
-
-        def SI(eg, t):
-            if ("s", eg) not in live:
-                si_new = work.tile([128, 512, 4], BF16, tag="si", bufs=2, align_bytes=64)
-                live["s", eg] = si_new
-            src = samp_raw[:, :, 512 * eg : 512 * (eg + 1)].rearrange("p j (q t r) -> p t q r j", t=4, r=8)
-            dst = live["s", eg][:].rearrange("p (t q r) j -> p t q r j", t=4, r=8)
-            nc.scalar.copy(dst[:, t], src[:, t])
-
-        def SQ(eg):
-            quant(live["s", eg][:].rearrange("p n j -> p (n j)"), sq[eg,][:], sqs[eg,][:])
-
-        def AM(j, eg, t):
-            acc = psum.tile([128, 512], F32, tag="acc", bufs=3)
-            s = slice(128 * t, 128 * (t + 1))
-            nc.tensor.matmul_mx(
-                out=acc[:], lhsT=sq[eg,][:, s].bitcast(FP8X4), lhsT_scale=sqs[eg,][:, s],
-                rhs=mq[j,][:].bitcast(FP8X4), rhs_scale=mqs[j,][:], start=True, stop=True,
+        def lift(key, operand, h):
+            cols = work_tile(("in", *operand), [128, 512, 4], BF16, "operand")[:, 256 * h : 256 * (h + 1), :]
+            nc.scalar.copy(
+                cols.rearrange("p n t -> p (n t)").bitcast(F32).rearrange("p (n r u) -> p n r u", n=2, u=2),
+                live[key][:].rearrange("p n u r -> p n r u"),
             )
-            live["a", j, eg, t] = acc
+            give_bank(key)
 
-        def YM(c, eg, t):
-            acc = psum.tile([128, 512], F32, tag="acc", bufs=3)
+        def lift_x(c, h, g):
+            lift(("xt", c, h, g), ("x", c, g), h)
+
+        def lift_modes(j, h):
+            lift(("mt", j, h), ("modes", j), h)
+
+        def interleave_samp(eg, t):
+            dst = work_tile(("in", "samp", eg), [128, 512, 4], BF16, "operand")
+            src = samp_raw[:, :, 512 * eg : 512 * (eg + 1)].rearrange("p j (q t r) -> p t q r j", t=4, r=8)
+            nc.scalar.copy(dst[:].rearrange("p (t q r) j -> p t q r j", t=4, r=8)[:, t], src[:, t])
+
+        def quantize(*key):
+            nc.vector.quantize_mx(
+                out=codes[key][:].bitcast(FP8X4), scales=planes[key][:],
+                in_=live["in", *key][:].rearrange("p n t -> p (n t)"),
+            )
+
+        def multiply_a(j, eg, t):
+            acc = take_bank(("a", j, eg, t), [128, 512], F32)
+            cols = slice(128 * t, 128 * (t + 1))
+            nc.tensor.matmul_mx(
+                out=acc[:], lhsT=codes["samp", eg][:, cols].bitcast(FP8X4), lhsT_scale=planes["samp", eg][:, cols],
+                rhs=codes["modes", j][:].bitcast(FP8X4), rhs_scale=planes["modes", j][:], start=True, stop=True,
+            )
+
+        def multiply_y(c, eg, t):
+            acc = take_bank(("y", c, eg, t), [128, 512], F32)
             e0 = 512 * eg + 128 * t
             for g in range(2):
                 nc.tensor.matmul_mx(
                     out=acc[:], lhsT=words[:, g, 2 * e0 : 2 * (e0 + 128)].bitcast(FP4X4),
                     lhsT_scale=scales[:, g, e0 : e0 + 128],
-                    rhs=xq[c, g][:].bitcast(FP8X4), rhs_scale=xqs[c, g][:],
+                    rhs=codes["x", c, g][:].bitcast(FP8X4), rhs_scale=planes["x", c, g][:],
                     start=(g == 0), stop=(g == 1),
                 )
-            live["y", c, eg, t] = acc
 
-        def empty(kind, i, eg, t):
-            key = kind + "raw", i, eg
-            if key not in live:
-                raw_new = work.tile([128, 2048], BF16, tag="raw", bufs=4, align_bytes=64)
-                live[key] = raw_new
-            raw = live[key]
-            if (kind, i, eg) in PAIR:
+        def empty(kind, n, eg, t):
+            raw = work_tile(("raw", kind, n, eg), [128, 2048], BF16, "raw")
+            if (kind, n, eg) in PAIRS_FIRST:
                 dst = raw[:].rearrange("p (u n e) -> p u n e", u=2, e=2)[:, t // 2, :, t % 2]
             else:
                 dst = raw[:, 512 * t : 512 * (t + 1)]
-            acc = live[kind, i, eg, t]
-            col = 8 * eg + t
+            acc = live[kind, n, eg, t]
             if kind == "y":
-                nc.scalar.activation(out=dst, in_=acc[:], func=ACT.Identity, bias=cols[:, col : col + 1], scale=1.0)
+                nc.scalar.activation(out=dst, in_=acc[:], func=ACT.Identity, bias=vec_cols[:, eg, t : t + 1], scale=1.0)
             else:
-                nc.scalar.activation(out=dst, in_=acc[:], func=ACT.Copy, scale=cols[:, col + 4 : col + 5])
+                nc.scalar.activation(out=dst, in_=acc[:], func=ACT.Copy, scale=vec_cols[:, eg, 4 + t : 5 + t])
+            give_bank((kind, n, eg, t))
 
-        def AS(j, eg, t):
-            empty("a", j, eg, t)
-
-        def YS(c, eg, t):
-            empty("y", c, eg, t)
-
-        def weave(kind, i, eg):
-            raw = live[kind + "raw", i, eg]
-            lay = work.tile([128, 2048], BF16, tag="lay", bufs=4, align_bytes=64)
-            if (kind, i, eg) in PAIR:
+        def interleave(kind, n, eg):
+            raw = live["raw", kind, n, eg]
+            dst = work_tile(("in", kind, n, eg), [128, 512, 4], BF16, "operand_ya")
+            if (kind, n, eg) in PAIRS_FIRST:
                 nc.vector.tensor_copy(
-                    out=lay[:].bitcast(F32).rearrange("p (n u) -> p n u", u=2),
+                    out=dst[:].rearrange("p n t -> p (n t)").bitcast(F32).rearrange("p (n u) -> p n u", u=2),
                     in_=raw[:].bitcast(F32).rearrange("p (u n) -> p n u", u=2),
                 )
             else:
                 nc.vector.tensor_copy(
-                    out=lay[:].rearrange("p (c i t) -> p c t i", i=4, t=4), in_=raw[:].rearrange("p (t c i) -> p c t i", t=4, i=4)
+                    out=dst[:].rearrange("p (c n) t -> p c t n", n=4),
+                    in_=raw[:].rearrange("p (t c n) -> p c t n", t=4, n=4),
                 )
-            live[kind + "lay", i, eg] = lay
 
-        def AI(j, eg):
-            weave("a", j, eg)
-
-        def YI(c, eg):
-            weave("y", c, eg)
-
-        def AQ(j, eg):
-            quant(live["alay", j, eg][:], aq[j, eg][:], aqs[j, eg][:])
-
-        def YQ(c, eg):
-            quant(live["ylay", c, eg][:], yq[c, eg][:], yqs[c, eg][:])
-
-        out_rows = out.rearrange("(c p i) d -> c p i d", p=128, i=4)
-
-        def ZM(c, i, j):
-            acc = psum.tile([128, 512], F32, tag="z", bufs=3)
-            s = slice(128 * i, 128 * (i + 1))
+        def multiply_z(c, i, j):
+            acc = take_bank(("z", c, i, j), [128, 512], F32)
+            cols = slice(128 * i, 128 * (i + 1))
             for eg in range(2):
                 nc.tensor.matmul_mx(
-                    out=acc[:], lhsT=yq[c, eg][:, s].bitcast(FP8X4), lhsT_scale=yqs[c, eg][:, s],
-                    rhs=aq[j, eg][:].bitcast(FP8X4), rhs_scale=aqs[j, eg][:], start=(eg == 0), stop=(eg == 1),
+                    out=acc[:], lhsT=codes["y", c, eg][:, cols].bitcast(FP8X4), lhsT_scale=planes["y", c, eg][:, cols],
+                    rhs=codes["a", j, eg][:].bitcast(FP8X4), rhs_scale=planes["a", j, eg][:],
+                    start=(eg == 0), stop=(eg == 1),
                 )
-            live["z", c, i, j] = acc
 
-        def ZC(c, i, j):
-            zc = work.tile([128, 512], F32, tag="zc", bufs=3)
-            nc.scalar.copy(zc[:], live["z", c, i, j][:])
-            live["z", c, i, j] = zc
+        def by_direction(tile):
+            return tile[:].rearrange("p (r i) -> p r i", i=4)
 
-        def ZT(c, i, j):
-            d0 = 512 * j
-            res = work.tile([128, 512], F32, tag="res", bufs=6)
-            if (c, i, j) == LAST:
-                for n in (slice(0, 256), slice(256, 512)):
-                    dn = slice(d0 + n.start, d0 + n.stop)
-                    nc.vector.tensor_tensor(out=res[:, n], in0=live["z", c, i, j][:, n], in1=norm_b[:, dn], op=ALU.mult)
-                    nc.sync.dma_start(out=out_rows[c, :, i, dn], in_=res[:, n])
-                return
-            engine = nc.gpsimd if (c, i, j) in ((2, 1, 0), (2, 1, 1), (2, 2, 1),) else nc.vector
-            engine.tensor_tensor(out=res[:], in0=live["z", c, i, j][:], in1=norm_b[:, d0 : d0 + 512], op=ALU.mult)
-            nc.sync.dma_start(out=out_rows[c, :, i, d0 : d0 + 512], in_=res[:])
+        def copy_z(c, i, j):
+            copied = work_tile(("copied", c, i, j), [128, 512], F32, "copied")
+            nc.scalar.copy(by_direction(copied), live["z", c, i, j][:].rearrange("p (i r) -> p r i", i=4))
+            give_bank(("z", c, i, j))
 
-        ops = {
-            "TT": TT, "TX": TX, "XS": XS, "XQ": XQ, "TM": TM, "MS": MS, "MQ": MQ, "SI": SI, "SQ": SQ, "AM": AM, "AS": AS,
-            "AI": AI, "AQ": AQ, "YM": YM, "YS": YS, "YI": YI, "YQ": YQ, "ZM": ZM, "ZC": ZC, "ZT": ZT, "CP": CP, "CS": CSP, "XB": XB, "XC": XC, "VT": VT, "VC": VC,
-        }
-        for op in ORDER.split():
-            ops[op[:2]](*[int(v) for v in op[2:].replace("P", "")])
+        def finish_z(c, i, j):
+            tile = (c, i, j)
+            result = work_tile(("result", *tile), [128, 512], F32, "result")
+            if tile in SHARED:
+                engine, src = nc.gpsimd, by_direction(live["copied", c, i, j])
+            else:
+                engine, src = nc.vector, live["z", c, i, j][:].rearrange("p (i r) -> p r i", i=4)
+            parts = 2 if tile == LAST else 1
+            rows = out.rearrange("(c p i) d -> c p i d", p=128, i=4)[c, :, i, 512 * j : 512 * (j + 1)]
+            for n in range(parts):
+                r = slice(128 // parts * n, 128 // parts * (n + 1))
+                d = slice(4 * r.start, 4 * r.stop)
+                factor = by_direction(norm_b)[:, 128 * j + r.start : 128 * j + r.stop, :]
+                engine.tensor_tensor(out=by_direction(result)[:, r, :], in0=src[:, r, :], in1=factor, op=ALU.mult)
+                nc.sync.dma_start(out=rows[:, d], in_=result[:, d])
+            if tile not in SHARED:
+                give_bank(("z", c, i, j))
+
+        def step(function, *args, needs=(), gives=None, banks=0):
+            return (function, args, needs, gives, banks)
+
+        def widens(c):
+            return [step(widen, c, i, needs=[("scales", 0), ("scales", 1)], gives=("xb", c, i)) for i in range(4)]
+
+        def turns_x(c, h):
+            return [step(turn_x, c, h, needs=[("xb", c, 2 * h), ("xb", c, 2 * h + 1)], gives=("xt", c, h), banks=2)]
+
+        def lifts_x(c):
+            return [
+                step(lift_x, c, h, g, needs=[("xt", c, h)], gives=("xl", c, h, g)) for h in range(2) for g in range(2)
+            ]
+
+        def quantizes_x(c):
+            return [
+                step(quantize, "x", c, g, needs=[("xl", c, h, g) for h in range(2)], gives=("x", c, g)) for g in range(2)
+            ]
+
+        def turns_modes(j):
+            return [step(turn_modes, j, gives=("mt", j), banks=2)]
+
+        def lifts_modes(j):
+            return [step(lift_modes, j, h, needs=[("mt", j)], gives=("ml", j, h)) for h in range(2)]
+
+        def quantizes_modes(j):
+            return [step(quantize, "modes", j, needs=[("ml", j, h) for h in range(2)], gives=("modes", j))]
+
+        def interleaves_samp(eg):
+            return [step(interleave_samp, eg, t, gives=("si", eg, t)) for t in range(4)]
+
+        def quantizes_samp(eg):
+            return [step(quantize, "samp", eg, needs=[("si", eg, t) for t in range(4)], gives=("samp", eg))]
+
+        def multiplies(kind, n, eg):
+            if kind == "a":
+                function, needs = multiply_a, [("samp", eg), ("modes", n)]
+            else:
+                function, needs = multiply_y, ["words", "scale_bytes", ("x", n, 0), ("x", n, 1)]
+            return [step(function, n, eg, t, needs=needs, gives=(kind, n, eg, t), banks=1) for t in range(4)]
+
+        def empties(kind, n, eg):
+            return [
+                step(empty, kind, n, eg, t, needs=[(kind, n, eg, t), "vec_cols"], gives=("e", kind, n, eg, t))
+                for t in range(4)
+            ]
+
+        def interleaves(kind, n, eg):
+            return [
+                step(interleave, kind, n, eg, needs=[("e", kind, n, eg, t) for t in range(4)], gives=("i", kind, n, eg))
+            ]
+
+        def quantizes(kind, n, eg):
+            return [step(quantize, kind, n, eg, needs=[("i", kind, n, eg)], gives=(kind, n, eg))]
+
+        def multiplies_z(tiles):
+            return [
+                step(
+                    multiply_z, *tile, gives=("z", *tile), banks=1,
+                    needs=[("y", tile[0], eg) for eg in range(2)] + [("a", tile[2], eg) for eg in range(2)],
+                )
+                for tile in tiles
+            ]
+
+        def copies_z(tiles):
+            return [step(copy_z, *tile, needs=[("z", *tile)], gives=("c", *tile)) for tile in tiles]
+
+        def finishes_z(tiles):
+            return [
+                step(finish_z, *tile, needs=[("c", *tile) if tile in SHARED else ("z", *tile)]) for tile in tiles
+            ]
+
+        z_first = [(0, i, 0) for i in range(4)]
+        z_second = [(1, i, 0) for i in range(3)]
+        z_rest = [(0, i, 1) for i in range(4)] + [(1, i, 1) for i in range(3)] + [(1, 3, 0), (1, 3, 1)]
+        z_rest += [(2, i, j) for i in range(4) for j in range(2)]
+        z_vector = [tile for tile in z_first + z_second + z_rest if tile not in SHARED]
+
+        tensor = [step(spread_scales, gives="xsc", banks=2)]
+        tensor += turns_modes(0) + turns_x(0, 0) + turns_x(0, 1)
+        tensor += [step(turn_vecs, gives="vecs", banks=1)]
+        tensor += turns_modes(1) + turns_x(1, 0) + turns_x(1, 1)
+        tensor += multiplies("a", 0, 0) + multiplies("a", 0, 1)
+        tensor += multiplies("y", 0, 0) + multiplies("y", 0, 1) + multiplies("y", 1, 0) + multiplies("y", 1, 1)
+        tensor += turns_x(2, 0) + turns_x(2, 1)
+        tensor += multiplies("a", 1, 0) + multiplies_z(z_first) + multiplies("a", 1, 1)
+        tensor += multiplies("y", 2, 0) + multiplies_z(z_second) + multiplies("y", 2, 1) + multiplies_z(z_rest)
+
+        scalar = [step(spread_out, 0, needs=["xsc"], gives=("scales", 0))]
+        scalar += interleaves_samp(0) + lifts_modes(0) + interleaves_samp(1)
+        scalar += lifts_x(0) + lifts_modes(1) + lifts_x(1)
+        scalar += [step(vecs_out, needs=["vecs"], gives="vec_cols")]
+        scalar += empties("a", 0, 0) + empties("a", 0, 1)
+        scalar += empties("y", 0, 0) + empties("y", 0, 1) + empties("y", 1, 0) + empties("y", 1, 1)
+        scalar += lifts_x(2) + empties("a", 1, 0) + empties("a", 1, 1)
+        scalar += empties("y", 2, 0) + copies_z(SHARED[:2]) + empties("y", 2, 1) + copies_z(SHARED[2:])
+
+        vector = [step(spread_out, 1, needs=["xsc"], gives=("scales", 1))]
+        vector += widens(0) + widens(1) + quantizes_modes(0)
+        vector += [step(permute_scales, gives="scale_bytes")]
+        vector += quantizes_samp(0) + quantizes_samp(1)
+        vector += [step(permute_words, gives="words")]
+        vector += quantizes_x(0) + quantizes_x(1) + widens(2) + quantizes_modes(1)
+        vector += interleaves("a", 0, 0) + interleaves("a", 0, 1) + interleaves("y", 0, 0) + interleaves("y", 0, 1)
+        vector += quantizes("a", 0, 0) + quantizes("a", 0, 1) + quantizes("y", 0, 0) + quantizes("y", 0, 1)
+        vector += interleaves("y", 1, 0) + interleaves("y", 1, 1) + quantizes_x(2) + finishes_z(z_vector[:2])
+        vector += quantizes("y", 1, 0) + quantizes("y", 1, 1) + interleaves("a", 1, 0) + interleaves("a", 1, 1)
+        vector += quantizes("a", 1, 0) + quantizes("a", 1, 1) + interleaves("y", 2, 0) + finishes_z(z_vector[2:7])
+        vector += quantizes("y", 2, 0) + interleaves("y", 2, 1) + finishes_z(z_vector[7:9])
+        vector += quantizes("y", 2, 1) + finishes_z(z_vector[9:])
+
+        queues = {"vector": vector, "scalar": scalar, "gpsimd": finishes_z(SHARED), "tensor": tensor}
+        at = {name: 0 for name in queues}
+        written = set()
+        while any(at[name] < len(queues[name]) for name in queues):
+            before = sum(at[name] for name in queues)
+            for name in queues:
+                for step_in_turn in queues[name][at[name] : at[name] + TURN[name]]:
+                    function, args, needs, gives, banks = step_in_turn
+                    if banks > len(free_banks) or any(need not in written for need in needs):
+                        break
+                    function(*args)
+                    written.add(gives)
+                    at[name] += 1
+            assert sum(at[name] for name in queues) > before

from contextlib import ExitStack

import concourse.mybir as mybir
from concourse.masks import make_identity

L, M, E, P, D = 1536, 1024, 1024, 512, 1024
FLOPS = 2 * L * M * E + 2 * D * P * E + 2 * L * E * D

F32 = mybir.dt.float32
BF16 = mybir.dt.bfloat16
U32 = mybir.dt.uint32
I32 = mybir.dt.int32
U8 = mybir.dt.uint8
FP8 = mybir.dt.float8_e4m3fn
FP8X4 = mybir.dt.float8_e4m3fn_x4
FP4X4 = mybir.dt.float4_e2m1fn_x4
ACT = mybir.ActivationFunctionType
ALU = mybir.AluOpType

CHUNKS = 3
BANKS = 8
PAIRS_FIRST = (("y", 2, 1),)
SHARED = ((1, 0, 0), (1, 1, 0), (0, 3, 1), (1, 2, 1))
LAST = (2, 3, 1)
BUFS = {"xb": 6, "operand": 10, "raw": 5, "operand_ya": 5, "copied": 4, "result": 6}
TURN = {"vector": 3, "scalar": 3, "gpsimd": 1, "tensor": 2}


def tile_coupling_compensated_beams_s11_kernel(
    tc, x_bytes, x_scale, cinv_words, cinv_scales, offset, modes, samp, taper, norm, out
):
    nc = tc.nc
    with ExitStack() as ctx:
        ctx.enter_context(tc.manual_schedule())
        keep = ctx.enter_context(tc.tile_pool(name="keep", bufs=1))
        work = ctx.enter_context(tc.tile_pool(name="work", bufs=1))
        psum = ctx.enter_context(tc.psum_pool(name="psum", bufs=1))

        ident = keep.tile([128, 128], F32, align_bytes=64)
        make_identity(nc, ident[:])
        scales_raw = keep.tile([128, 2, E], U8, align_bytes=64)
        nc.vector.memset(scales_raw[:].bitcast(I32), 0)
        vecs = keep.tile([128, 256], BF16, align_bytes=64)
        nc.gpsimd.memset(vecs[:], 0.0)
        ident_b = keep.tile([128, 128], BF16, align_bytes=64)
        make_identity(nc, ident_b[:])

        scale_cols = keep.tile([128, 8], F32, align_bytes=64)
        samp_raw = keep.tile([128, 4, E], BF16, align_bytes=64)
        words_raw = keep.tile([128, 2, 2 * E], U8, align_bytes=64)
        norm_b = keep.tile([128, D], BF16, align_bytes=64)
        modes_raw = [keep.tile([128, 4, P], BF16, name=f"modes_raw_{j}", align_bytes=64) for j in range(2)]
        x_row = {}

        def load_x(c, first, count):
            x_raw = keep.tile([128, count, M], U8, name=f"x_raw_{c}_{first}", align_bytes=64)
            rows = x_bytes.rearrange("(c p i) k -> c p i k", p=128, i=4)
            nc.sync.dma_start(out=x_raw[:], in_=rows[c, :, first : first + count, :])
            for n in range(count):
                x_row[c, first + n] = x_raw[:, n, :]

        def load_samp(eg):
            cols = slice(512 * eg, 512 * (eg + 1))
            nc.sync.dma_start(out=samp_raw[:, :, cols], in_=samp.rearrange("(p j) e -> p j e", j=4)[:, :, cols])

        def load_modes(j):
            rows = modes[512 * j : 512 * (j + 1), :]
            nc.sync.dma_start(out=modes_raw[j][:], in_=rows.rearrange("(p i) k -> p i k", i=4))

        nc.sync.dma_start(out=scale_cols[:], in_=x_scale.rearrange("o (p c) -> p (o c)", c=8))
        load_samp(0)
        load_x(0, 0, 2)
        load_modes(0)
        load_x(0, 2, 2)
        load_samp(1)
        for n, vec in enumerate((offset, taper)):
            nc.sync.dma_start(
                out=vecs[4 * n : 4 * n + 4, :].rearrange("t (a r) -> t a r", r=8),
                in_=vec.rearrange("(a t r) -> t a r", t=4, r=8),
            )
        load_x(1, 0, 4)
        for n in range(4):
            nc.sync.dma_start(
                out=scales_raw[32 * n : 32 * n + 4, :, :].bitcast(I32),
                in_=cinv_scales[:, 4 * n : 4 * n + 4, :].rearrange("g r n -> r g n").bitcast(I32),
            )
        load_modes(1)
        nc.sync.dma_start(out=words_raw[:].bitcast(I32), in_=cinv_words.rearrange("g p n -> p g n").bitcast(I32))
        load_x(2, 0, 4)
        nc.sync.dma_start(out=norm_b[:], in_=norm.partition_broadcast(128))

        xsc = keep.tile([128, M], F32, align_bytes=64)
        vec_cols = keep.tile([128, 2, 8], F32, align_bytes=64)
        words = keep.tile([128, 2, 2 * E], U8, align_bytes=64)
        scales = keep.tile([128, 2, E], U8, align_bytes=64)
        codes = {}
        planes = {}
        keys = [("x", c, g) for c in range(CHUNKS) for g in range(2)] + [("modes", j) for j in range(2)]
        keys += [("samp", eg) for eg in range(2)] + [("a", j, eg) for j in range(2) for eg in range(2)]
        keys += [("y", c, eg) for c in range(CHUNKS) for eg in range(2)]
        for n, key in enumerate(keys):
            codes[key] = keep.tile([128, 512], U32, name=f"codes_{n}", align_bytes=64)
            planes[key] = keep.tile([128, 512], U8, name=f"planes_{n}", align_bytes=64)

        free_banks = list(range(BANKS))
        bank_of = {}
        live = {}

        def take_bank(key, shape, dtype):
            b = free_banks[0]
            free_banks.remove(b)
            bank = psum.tile(shape, dtype, name=f"bank_{b}", tag=f"bank_{b}", bufs=1)
            bank_of[key] = b
            live[key] = bank
            return bank

        def give_bank(key):
            free_banks.extend([bank_of[key]])

        def work_tile(key, shape, dtype, tag):
            if key not in live:
                made = work.tile(shape, dtype, name=tag, tag=tag, bufs=BUFS[tag], align_bytes=64)
                live[key] = made
            return live[key]

        def spread_scales():
            for b in range(2):
                bank = take_bank(("xsc", b), [128, 4, 128], F32)
                for n in range(4):
                    col = scale_cols[:, 4 * b + n : 4 * b + n + 1]
                    nc.tensor.transpose(bank[:, n, :], col.to_broadcast([128, 128]), ident[:])

        def spread_out(b):
            dst = xsc[:].rearrange("p (k c) -> p k c", c=8)[:, :, 4 * b : 4 * b + 4]
            src = live["xsc", b][:].rearrange("p c k -> p k c")
            if b == 0:
                nc.scalar.copy(dst, src)
            else:
                nc.vector.tensor_copy(out=dst, in_=src)
            give_bank(("xsc", b))

        def turn_vecs():
            bank = take_bank("vecs", [128, 2, 128], BF16)
            for eg in range(2):
                nc.tensor.transpose(bank[:, eg, :], vecs[:, 128 * eg : 128 * (eg + 1)], ident_b[:])

        def vecs_out():
            nc.scalar.copy(vec_cols[:], live["vecs"][:, :, 0:8])
            give_bank("vecs")

        def permute(dst, src, w):
            nc.vector.tensor_copy(
                out=dst[:].rearrange("p g n -> p (g n)").bitcast(I32).rearrange("p (a t q w) -> p a t q w", a=4, t=4, w=w),
                in_=src[:].rearrange("p g n -> p (g n)").bitcast(I32).rearrange("p (a q t w) -> p a t q w", a=4, t=4, w=w),
            )

        def permute_words():
            permute(words, words_raw, 4)

        def permute_scales():
            permute(scales, scales_raw, 2)

        def widen(c, i):
            xb = work_tile(("xb", c, i // 2), [128, 2, M], BF16, "xb")
            nc.vector.tensor_tensor(out=xb[:, i % 2, :], in0=x_row[c, i].bitcast(FP8), in1=xsc[:], op=ALU.mult)

        def turn(key, rows, k0):
            bank = take_bank(key, [128, 2, 2, 128], F32)
            for n in range(2):
                row_words = rows[n].bitcast(F32)
                for u in range(2):
                    nc.tensor.transpose(bank[:, n, u, :], row_words[:, k0 + u : k0 + 256 : 2], ident[:])

        def turn_x(c, h):
            xb = live["xb", c, h]
            for g in range(2):
                turn(("xt", c, h, g), [xb[:, n, :] for n in range(2)], 256 * g)

        def turn_modes(j):
            for h in range(2):
                turn(("mt", j, h), [modes_raw[j][:, 2 * h + n, :] for n in range(2)], 0)

        def lift(key, operand, h):
            cols = work_tile(("in", *operand), [128, 512, 4], BF16, "operand")[:, 256 * h : 256 * (h + 1), :]
            nc.scalar.copy(
                cols.rearrange("p n t -> p (n t)").bitcast(F32).rearrange("p (n r u) -> p n r u", n=2, u=2),
                live[key][:].rearrange("p n u r -> p n r u"),
            )
            give_bank(key)

        def lift_x(c, h, g):
            lift(("xt", c, h, g), ("x", c, g), h)

        def lift_modes(j, h):
            lift(("mt", j, h), ("modes", j), h)

        def interleave_samp(eg, t):
            dst = work_tile(("in", "samp", eg), [128, 512, 4], BF16, "operand")
            src = samp_raw[:, :, 512 * eg : 512 * (eg + 1)].rearrange("p j (q t r) -> p t q r j", t=4, r=8)
            nc.scalar.copy(dst[:].rearrange("p (t q r) j -> p t q r j", t=4, r=8)[:, t], src[:, t])

        def quantize(*key):
            nc.vector.quantize_mx(
                out=codes[key][:].bitcast(FP8X4), scales=planes[key][:],
                in_=live["in", *key][:].rearrange("p n t -> p (n t)"),
            )

        def multiply_a(j, eg, t):
            acc = take_bank(("a", j, eg, t), [128, 512], F32)
            cols = slice(128 * t, 128 * (t + 1))
            nc.tensor.matmul_mx(
                out=acc[:], lhsT=codes["samp", eg][:, cols].bitcast(FP8X4), lhsT_scale=planes["samp", eg][:, cols],
                rhs=codes["modes", j][:].bitcast(FP8X4), rhs_scale=planes["modes", j][:], start=True, stop=True,
            )

        def multiply_y(c, eg, t):
            acc = take_bank(("y", c, eg, t), [128, 512], F32)
            e0 = 512 * eg + 128 * t
            for g in range(2):
                nc.tensor.matmul_mx(
                    out=acc[:], lhsT=words[:, g, 2 * e0 : 2 * (e0 + 128)].bitcast(FP4X4),
                    lhsT_scale=scales[:, g, e0 : e0 + 128],
                    rhs=codes["x", c, g][:].bitcast(FP8X4), rhs_scale=planes["x", c, g][:],
                    start=(g == 0), stop=(g == 1),
                )

        def empty(kind, n, eg, t):
            raw = work_tile(("raw", kind, n, eg), [128, 2048], BF16, "raw")
            if (kind, n, eg) in PAIRS_FIRST:
                dst = raw[:].rearrange("p (u n e) -> p u n e", u=2, e=2)[:, t // 2, :, t % 2]
            else:
                dst = raw[:, 512 * t : 512 * (t + 1)]
            acc = live[kind, n, eg, t]
            if kind == "y":
                nc.scalar.activation(out=dst, in_=acc[:], func=ACT.Identity, bias=vec_cols[:, eg, t : t + 1], scale=1.0)
            else:
                nc.scalar.activation(out=dst, in_=acc[:], func=ACT.Copy, scale=vec_cols[:, eg, 4 + t : 5 + t])
            give_bank((kind, n, eg, t))

        def interleave(kind, n, eg):
            raw = live["raw", kind, n, eg]
            dst = work_tile(("in", kind, n, eg), [128, 512, 4], BF16, "operand_ya")
            if (kind, n, eg) in PAIRS_FIRST:
                nc.vector.tensor_copy(
                    out=dst[:].rearrange("p n t -> p (n t)").bitcast(F32).rearrange("p (n u) -> p n u", u=2),
                    in_=raw[:].bitcast(F32).rearrange("p (u n) -> p n u", u=2),
                )
            else:
                nc.vector.tensor_copy(
                    out=dst[:].rearrange("p (c n) t -> p c t n", n=4),
                    in_=raw[:].rearrange("p (t c n) -> p c t n", t=4, n=4),
                )

        def multiply_z(c, i, j):
            acc = take_bank(("z", c, i, j), [128, 512], F32)
            cols = slice(128 * i, 128 * (i + 1))
            for eg in range(2):
                nc.tensor.matmul_mx(
                    out=acc[:], lhsT=codes["y", c, eg][:, cols].bitcast(FP8X4), lhsT_scale=planes["y", c, eg][:, cols],
                    rhs=codes["a", j, eg][:].bitcast(FP8X4), rhs_scale=planes["a", j, eg][:],
                    start=(eg == 0), stop=(eg == 1),
                )

        def by_direction(tile):
            return tile[:].rearrange("p (r i) -> p r i", i=4)

        def copy_z(c, i, j):
            copied = work_tile(("copied", c, i, j), [128, 512], F32, "copied")
            nc.scalar.copy(by_direction(copied), live["z", c, i, j][:].rearrange("p (i r) -> p r i", i=4))
            give_bank(("z", c, i, j))

        def finish_z(c, i, j):
            tile = (c, i, j)
            result = work_tile(("result", *tile), [128, 512], F32, "result")
            if tile in SHARED:
                engine, src = nc.gpsimd, by_direction(live["copied", c, i, j])
            else:
                engine, src = nc.vector, live["z", c, i, j][:].rearrange("p (i r) -> p r i", i=4)
            parts = 2 if tile == LAST else 1
            rows = out.rearrange("(c p i) d -> c p i d", p=128, i=4)[c, :, i, 512 * j : 512 * (j + 1)]
            for n in range(parts):
                r = slice(128 // parts * n, 128 // parts * (n + 1))
                d = slice(4 * r.start, 4 * r.stop)
                factor = by_direction(norm_b)[:, 128 * j + r.start : 128 * j + r.stop, :]
                engine.tensor_tensor(out=by_direction(result)[:, r, :], in0=src[:, r, :], in1=factor, op=ALU.mult)
                nc.sync.dma_start(out=rows[:, d], in_=result[:, d])
            if tile not in SHARED:
                give_bank(("z", c, i, j))

        def step(function, *args, needs=(), gives=None, banks=0):
            return (function, args, needs, gives, banks)

        def widens(c):
            return [step(widen, c, i, needs=[("scales", 0), ("scales", 1)], gives=("xb", c, i)) for i in range(4)]

        def turns_x(c, h):
            return [step(turn_x, c, h, needs=[("xb", c, 2 * h), ("xb", c, 2 * h + 1)], gives=("xt", c, h), banks=2)]

        def lifts_x(c):
            return [
                step(lift_x, c, h, g, needs=[("xt", c, h)], gives=("xl", c, h, g)) for h in range(2) for g in range(2)
            ]

        def quantizes_x(c):
            return [
                step(quantize, "x", c, g, needs=[("xl", c, h, g) for h in range(2)], gives=("x", c, g)) for g in range(2)
            ]

        def turns_modes(j):
            return [step(turn_modes, j, gives=("mt", j), banks=2)]

        def lifts_modes(j):
            return [step(lift_modes, j, h, needs=[("mt", j)], gives=("ml", j, h)) for h in range(2)]

        def quantizes_modes(j):
            return [step(quantize, "modes", j, needs=[("ml", j, h) for h in range(2)], gives=("modes", j))]

        def interleaves_samp(eg):
            return [step(interleave_samp, eg, t, gives=("si", eg, t)) for t in range(4)]

        def quantizes_samp(eg):
            return [step(quantize, "samp", eg, needs=[("si", eg, t) for t in range(4)], gives=("samp", eg))]

        def multiplies(kind, n, eg):
            if kind == "a":
                function, needs = multiply_a, [("samp", eg), ("modes", n)]
            else:
                function, needs = multiply_y, ["words", "scale_bytes", ("x", n, 0), ("x", n, 1)]
            return [step(function, n, eg, t, needs=needs, gives=(kind, n, eg, t), banks=1) for t in range(4)]

        def empties(kind, n, eg):
            return [
                step(empty, kind, n, eg, t, needs=[(kind, n, eg, t), "vec_cols"], gives=("e", kind, n, eg, t))
                for t in range(4)
            ]

        def interleaves(kind, n, eg):
            return [
                step(interleave, kind, n, eg, needs=[("e", kind, n, eg, t) for t in range(4)], gives=("i", kind, n, eg))
            ]

        def quantizes(kind, n, eg):
            return [step(quantize, kind, n, eg, needs=[("i", kind, n, eg)], gives=(kind, n, eg))]

        def multiplies_z(tiles):
            return [
                step(
                    multiply_z, *tile, gives=("z", *tile), banks=1,
                    needs=[("y", tile[0], eg) for eg in range(2)] + [("a", tile[2], eg) for eg in range(2)],
                )
                for tile in tiles
            ]

        def copies_z(tiles):
            return [step(copy_z, *tile, needs=[("z", *tile)], gives=("c", *tile)) for tile in tiles]

        def finishes_z(tiles):
            return [
                step(finish_z, *tile, needs=[("c", *tile) if tile in SHARED else ("z", *tile)]) for tile in tiles
            ]

        z_first = [(0, i, 0) for i in range(4)]
        z_second = [(1, i, 0) for i in range(3)]
        z_rest = [(0, i, 1) for i in range(4)] + [(1, i, 1) for i in range(3)] + [(1, 3, 0), (1, 3, 1)]
        z_rest += [(2, i, j) for i in range(4) for j in range(2)]
        z_vector = [tile for tile in z_first + z_second + z_rest if tile not in SHARED]

        tensor = [step(spread_scales, gives="xsc", banks=2)]
        tensor += turns_modes(0) + turns_x(0, 0) + turns_x(0, 1)
        tensor += [step(turn_vecs, gives="vecs", banks=1)]
        tensor += turns_modes(1) + turns_x(1, 0) + turns_x(1, 1)
        tensor += multiplies("a", 0, 0) + multiplies("a", 0, 1)
        tensor += multiplies("y", 0, 0) + multiplies("y", 0, 1) + multiplies("y", 1, 0) + multiplies("y", 1, 1)
        tensor += turns_x(2, 0) + turns_x(2, 1)
        tensor += multiplies("a", 1, 0) + multiplies_z(z_first) + multiplies("a", 1, 1)
        tensor += multiplies("y", 2, 0) + multiplies_z(z_second) + multiplies("y", 2, 1) + multiplies_z(z_rest)

        scalar = [step(spread_out, 0, needs=["xsc"], gives=("scales", 0))]
        scalar += interleaves_samp(0) + lifts_modes(0) + interleaves_samp(1)
        scalar += lifts_x(0) + lifts_modes(1) + lifts_x(1)
        scalar += [step(vecs_out, needs=["vecs"], gives="vec_cols")]
        scalar += empties("a", 0, 0) + empties("a", 0, 1)
        scalar += empties("y", 0, 0) + empties("y", 0, 1) + empties("y", 1, 0) + empties("y", 1, 1)
        scalar += lifts_x(2) + empties("a", 1, 0) + empties("a", 1, 1)
        scalar += empties("y", 2, 0) + copies_z(SHARED[:2]) + empties("y", 2, 1) + copies_z(SHARED[2:])

        vector = [step(spread_out, 1, needs=["xsc"], gives=("scales", 1))]
        vector += widens(0) + widens(1) + quantizes_modes(0)
        vector += [step(permute_scales, gives="scale_bytes")]
        vector += quantizes_samp(0) + quantizes_samp(1)
        vector += [step(permute_words, gives="words")]
        vector += quantizes_x(0) + quantizes_x(1) + widens(2) + quantizes_modes(1)
        vector += interleaves("a", 0, 0) + interleaves("a", 0, 1) + interleaves("y", 0, 0) + interleaves("y", 0, 1)
        vector += quantizes("a", 0, 0) + quantizes("a", 0, 1) + quantizes("y", 0, 0) + quantizes("y", 0, 1)
        vector += interleaves("y", 1, 0) + interleaves("y", 1, 1) + quantizes_x(2) + finishes_z(z_vector[:2])
        vector += quantizes("y", 1, 0) + quantizes("y", 1, 1) + interleaves("a", 1, 0) + interleaves("a", 1, 1)
        vector += quantizes("a", 1, 0) + quantizes("a", 1, 1) + interleaves("y", 2, 0) + finishes_z(z_vector[2:7])
        vector += quantizes("y", 2, 0) + interleaves("y", 2, 1) + finishes_z(z_vector[7:9])
        vector += quantizes("y", 2, 1) + finishes_z(z_vector[9:])

        queues = {"vector": vector, "scalar": scalar, "gpsimd": finishes_z(SHARED), "tensor": tensor}
        at = {name: 0 for name in queues}
        written = set()
        while any(at[name] < len(queues[name]) for name in queues):
            before = sum(at[name] for name in queues)
            for name in queues:
                for step_in_turn in queues[name][at[name] : at[name] + TURN[name]]:
                    function, args, needs, gives, banks = step_in_turn
                    if banks > len(free_banks) or any(need not in written for need in needs):
                        break
                    function(*args)
                    written.add(gives)
                    at[name] += 1
            assert sum(at[name] for name in queues) > before
